import numpy as np
import ml_dtypes


def mxq(x, axis, fmt="e4m3"):
    dtype, down = {"e4m3": (ml_dtypes.float8_e4m3fn, 7), "e5m2": (ml_dtypes.float8_e5m2, 14)}[fmt]
    v = np.moveaxis(np.asarray(x, np.float32).astype(ml_dtypes.bfloat16).astype(np.float64), axis, -1)
    blocks = v.reshape(v.shape[:-1] + (-1, 32))
    amax = np.abs(blocks).max(-1, keepdims=True)
    byte = np.maximum(np.where(amax > 0, np.frexp(amax)[1] - 1 + 127, 0) - down, 1)
    scale = np.exp2(byte - 127.0)
    codes = (blocks / scale).astype(np.float32).astype(dtype).astype(np.float64)
    return np.moveaxis((codes * scale).reshape(v.shape), -1, axis)


WIDE = False


def mx_kscale(k):
    if not WIDE:
        return np.ones(k)
    levels = np.array([10, -10, 5, -5, 0])
    if k % 512:
        return np.exp2(np.random.permutation(np.resize(levels, k // 32))).repeat(32)
    a = np.empty((k // 512, 16))
    for p in range(k // 512):
        a[p, :8] = np.random.permutation(np.resize(levels, 8))
        for g in range(8):
            far = levels[np.abs(levels - a[p, g]) >= 10]
            a[p, g + 8] = far[np.random.randint(len(far))]
    return np.exp2(a.ravel()).repeat(32)


def f64(x):
    return np.asarray(x).astype(np.float64)


def striped(idx):
    return np.tile(idx.reshape(-1, 16).T, (8, 1)).astype(np.uint16)


def unstriped(offs):
    return offs[:16].T.reshape(-1).astype(np.int64)


def relu(v):
    return np.maximum(v, 0.0)


K, T, E, C, H, N = 1024, 512, 2, 256, 1024, 128


def by_expert(wq, xq):
    return np.concatenate([wq[e].T @ xq[:, e * C:(e + 1) * C] for e in range(E)], axis=1)


def setup_inputs():
    n = np.random.standard_normal
    s = mx_kscale(K)[:, None]
    u = mx_kscale(H)
    return {
        "xT": (n((K, T)) * s).astype(np.float32),
        "w1": (n((E, K, H)) / np.sqrt(K) / s[None]).astype(np.float32),
        "w3": (n((E, K, H)) / np.sqrt(K) / s[None] * u[None, None, :]).astype(np.float32),
        "w2": (n((E, H, N)) / np.sqrt(H) / u[None, :, None]).astype(np.float32),
        "gate": np.tile(np.random.uniform(0.2, 1.0, E * C), (K, 1)).astype(np.float32),
        "offs": striped(np.random.permutation(T)[:E * C]),
    }


def reference(xT, w1, w3, w2, gate, offs):
    idx = unstriped(offs)
    xq = mxq(f64(gate) * f64(xT)[:, idx], 0, "e4m3")
    h = relu(by_expert(mxq(f64(w1), 1, "e4m3"), xq))
    h = h * by_expert(mxq(f64(w3), 1, "e4m3"), xq)
    y = by_expert(mxq(f64(w2), 1, "e4m3"), mxq(h, 0, "e4m3"))
    out = np.zeros((N, T))
    out[:, idx] = y
    return out

@@ -1,0 +1,213 @@
+from contextlib import ExitStack
+
+import concourse.mybir as mybir
+
+K, T, E, C, H, N = 1024, 512, 2, 256, 1024, 128
+FLOPS = 2 * E * C * (2 * K * H + H * N)
+BYTES = 4 * (K * T + 2 * E * K * H + E * H * N + 128 * T + N * T) + 2 * 128 * 32
+
+F32 = mybir.dt.float32
+BF16 = mybir.dt.bfloat16
+U32 = mybir.dt.uint32
+U16 = mybir.dt.uint16
+U8 = mybir.dt.uint8
+FP8X4 = mybir.dt.float8_e4m3fn_x4
+MULT = mybir.AluOpType.mult
+MAX = mybir.AluOpType.max
+
+P = 128
+PACK = 4
+PASS = P * PACK
+KP = K // PASS
+HP = H // PASS
+HALF = 128
+HALVES = C // HALF
+LIST_COLS = 16
+
+SHARES = [104, 104, 104, 112, 40, 32, 80, 88, 120, 72, 32, 32, 72, 80, 64, 72]
+XQ = 0
+XCAST = [0, 0, 1, 1]
+W2CAST = [1, 0]
+SEQ = "xxxx 300c xxxx P00 301c 100c 101c P10 P01 P11 v0 310c 111a 110c 311a 311b 111b v1"
+QS = [1, 1, 4, 2, 1, 1, 2, 4, 1, 1, 1, 1, 1, 1, 1, 4]
+WB = 5
+BE = [1, 0, 0, 0, 0, 0, 0, 0]
+YE = [0, 0, 0, 1]
+RB = 5
+PB = 3
+
+
+def tile_moe_pre_glu_relu_kernel(tc, xT, w1, w3, w2, gate, offs, out):
+    nc = tc.nc
+    with ExitStack() as ctx:
+        keep = ctx.enter_context(tc.tile_pool(name="keep", bufs=1))
+        stream = ctx.enter_context(tc.tile_pool(name="stream", bufs=RB))
+        stage = ctx.enter_context(tc.tile_pool(name="stage", bufs=4))
+        psum = ctx.enter_context(tc.psum_pool(name="psum", bufs=PB))
+        psum_y = ctx.enter_context(tc.psum_pool(name="psum_y", bufs=2))
+
+        offsets = keep.tile([P, E * C // LIST_COLS], U16, name="offsets")
+        gate_sb = keep.tile([P, E * C], F32, name="gate_sb")
+        out_sb = keep.tile([P, T], F32, name="out_sb")
+        x_rows = {}
+        x_mx = {}
+        w_mx = {}
+        w2_mx = {}
+        b_sb = {}
+        h_mx = {}
+
+        def quantize(grouped, name, calls=1):
+            words = grouped.shape[1] // PACK
+            codes = keep.tile([P, words], U32, name=name + "_codes", align_bytes=64)
+            scales = keep.tile([P, words], U8, name=name + "_scales", align_bytes=64)
+            step = words // calls
+            for c in range(0, words, step):
+                nc.vector.quantize_mx(
+                    out=codes[:, c : c + step].bitcast(FP8X4),
+                    scales=scales[:, c : c + step],
+                    in_=grouped[:, c * PACK : (c + step) * PACK],
+                )
+            return codes, scales
+
+        def load_x(g, j):
+            rows = keep.tile([P, T], F32, name="x_rows_%d_%d" % (g, j))
+            src = xT[g * PASS : (g + 1) * PASS, :].rearrange("(p j) n -> p j n", j=PACK)
+            (nc.scalar if XQ else nc.sync).dma_start(out=rows[:], in_=src[:, j, :])
+            x_rows[g, j] = rows
+
+        def prepare_x(e, g):
+            slots = slice(e * C, (e + 1) * C)
+            entries = offsets[:, e * C // LIST_COLS : (e + 1) * C // LIST_COLS]
+            picked = stage.tile([P, PACK, C], F32, name="picked", bufs=2)
+            for j in range(PACK):
+                nc.vector.tensor_tensor(picked[:, j, :], x_rows[g, j][:].indirect(entries), gate_sb[:, slots], MULT)
+            grouped = stage.tile([P, C * PACK], BF16, name="x_grouped", align_bytes=64, bufs=2)
+            (nc.vector.tensor_copy if XCAST[2 * e + g] else nc.scalar.copy)(
+                out=grouped[:].rearrange("p (c i j) -> p c j i", i=4, j=PACK),
+                in_=picked[:].rearrange("p j (c i) -> p c j i", i=4),
+            )
+            x_mx[e, g] = quantize(grouped[:], "x_%d_%d" % (e, g))
+
+        def load_w(w, e, g, first, last):
+            cols = slice(first * PASS, last * PASS)
+            raw = stream.tile([P, PACK, (last - first) * PASS], F32, name="raw")
+            src = w[e, g * PASS : (g + 1) * PASS, :].rearrange("(p j) c -> p j c", j=PACK)
+            nc.sync.dma_start(out=raw[:], in_=src[:, :, cols])
+            return raw
+
+        def prepare_w(raw, which, e, g, first, last):
+            for q in range(first, last):
+                share = SHARES[8 * e + (4 if which == 1 else 0) + 2 * g + q]
+                grouped = stage.tile([P, PASS * PACK], BF16, name="w_grouped", align_bytes=64, bufs=WB)
+                dst = grouped[:].rearrange("p (t m j) -> p m j t", t=PACK, j=PACK)
+                src = raw[:, :, (q - first) * PASS : (q - first + 1) * PASS].rearrange("p j (m t) -> p m j t", t=PACK)
+                if share > 0:
+                    nc.scalar.copy(out=dst[:, :share], in_=src[:, :share])
+                if share < P:
+                    nc.vector.tensor_copy(out=dst[:, share:], in_=src[:, share:])
+                w_mx[which, e, g, q] = quantize(grouped[:], "w%d_%d_%d_%d" % (which, e, g, q), QS[8 * e + (4 if which == 1 else 0) + 2 * g + q])
+
+        def load_w2(e):
+            raw = stream.tile([P, HP, PACK * N], F32, name="raw")
+            nc.sync.dma_start(out=raw[:], in_=w2[e].rearrange("(q p j) n -> p q (j n)", p=P, j=PACK))
+            return raw
+
+        def prepare_w2(e, raw):
+            grouped = stage.tile([P, HP * N * PACK], BF16, name="w2_grouped", align_bytes=64, bufs=2)
+            (nc.vector.tensor_copy if W2CAST[e] else nc.scalar.copy)(
+                out=grouped[:].rearrange("p (q c i j) -> p q c j i", q=HP, i=4, j=PACK),
+                in_=raw[:].rearrange("p q (j c i) -> p q c j i", j=PACK, i=4),
+            )
+            w2_mx[e] = quantize(grouped[:], "w2_%d" % e)
+
+        def first_layer(which, e, q, s):
+            bank = psum.tile([P, PACK, HALF], F32, name="bank_%d" % which)
+            cols = slice(s * HALF, (s + 1) * HALF)
+            for t in range(PACK):
+                for g in range(KP):
+                    w_codes, w_scales = w_mx[which, e, g, q]
+                    x_codes, x_scales = x_mx[e, g]
+                    nc.tensor.matmul_mx(
+                        out=bank[:, t, :],
+                        lhsT=w_codes[:, t * P : (t + 1) * P].bitcast(FP8X4),
+                        lhsT_scale=w_scales[:, t * P : (t + 1) * P],
+                        rhs=x_codes[:, cols].bitcast(FP8X4),
+                        rhs_scale=x_scales[:, cols],
+                        start=(g == 0),
+                        stop=(g == KP - 1),
+                    )
+            return bank[:].rearrange("p t n -> p n t")
+
+        def linear_branch(e, q):
+            for s in range(HALVES):
+                sums = first_layer(3, e, q, s)
+                held = stage.tile([P, HALF, PACK], F32, name="b_held")
+                (nc.vector.tensor_copy if BE[4 * e + 2 * q + s] else nc.scalar.copy)(out=held[:], in_=sums)
+                b_sb[e, q, s] = held
+
+        def hidden(e, q):
+            for s in range(HALVES):
+                sums = first_layer(1, e, q, s)
+                grouped = stage.tile([P, HALF, PACK], BF16, name="h_grouped", align_bytes=64)
+                nc.vector.scalar_tensor_tensor(
+                    out=grouped[:], in0=sums, scalar=0.0, in1=b_sb[e, q, s][:], op0=MAX, op1=MULT
+                )
+                h_mx[e, q, s] = quantize(grouped[:].rearrange("p n t -> p (n t)"), "h_%d_%d_%d" % (e, q, s))
+
+        def second_layer(e):
+            w_codes, w_scales = w2_mx[e]
+            for s in range(HALVES):
+                bank = psum_y.tile([P, HALF], F32, name="bank_y")
+                for q in range(HP):
+                    h_codes, h_scales = h_mx[e, q, s]
+                    nc.tensor.matmul_mx(
+                        out=bank[:],
+                        lhsT=w_codes[:, q * N : (q + 1) * N].bitcast(FP8X4),
+                        lhsT_scale=w_scales[:, q * N : (q + 1) * N],
+                        rhs=h_codes[:].bitcast(FP8X4),
+                        rhs_scale=h_scales[:],
+                        start=(q == 0),
+                        stop=(q == HP - 1),
+                    )
+                y = stage.tile([P, HALF], F32, name="y")
+                (nc.vector.tensor_copy if YE[2 * e + s] else nc.scalar.copy)(out=y[:], in_=bank[:])
+                first = (e * C + s * HALF) // LIST_COLS
+                nc.vector.tensor_copy(out_sb[:].indirect(offsets[:, first : first + HALF // LIST_COLS]), y[:])
+
+        nc.sync.dma_start(offsets[:], offs)
+        (nc.scalar if XQ else nc.sync).dma_start(out=gate_sb[:], in_=gate[:P, :])
+        planes = [(g, j) for g in range(KP) for j in range(PACK)]
+        todo = []
+        for tok in SEQ.split():
+            if tok[0] == "x":
+                for r in range(len(tok)):
+                    load_x(*planes.pop(0))
+            elif tok[0] == "P":
+                todo.append(("P", int(tok[1]), int(tok[2])))
+            elif tok[0] == "v":
+                todo.append(("v", int(tok[1]), load_w2(int(tok[1]))))
+            else:
+                which, e, g = int(tok[0]), int(tok[1]), int(tok[2])
+                first, last = {"a": (0, 1), "b": (1, 2), "c": (0, 2)}[tok[3]]
+                todo.append(("w", which, e, g, first, last, load_w(w1 if which == 1 else w3, e, g, first, last)))
+        did = set()
+        for item in todo:
+            if item[0] == "P":
+                prepare_x(item[1], item[2])
+            elif item[0] == "v":
+                prepare_w2(item[1], item[2])
+            else:
+                prepare_w(item[6], *item[1:6])
+            for e in range(E):
+                ready_x = all((e, g) in x_mx for g in range(KP))
+                for q in range(HP):
+                    if ready_x and ("b", e, q) not in did and all((3, e, g, q) in w_mx for g in range(KP)):
+                        did.add(("b", e, q))
+                        linear_branch(e, q)
+                    if ("b", e, q) in did and ("h", e, q) not in did and all((1, e, g, q) in w_mx for g in range(KP)):
+                        did.add(("h", e, q))
+                        hidden(e, q)
+                if ("y", e) not in did and e in w2_mx and all(("h", e, q) in did for q in range(HP)):
+                    did.add(("y", e))
+                    second_layer(e)
+        nc.sync.dma_start(out=out, in_=out_sb[:])

@@ -24,17 +24,22 @@ HALF = 128
 HALVES = C // HALF
 LIST_COLS = 16
 
-SHARES = [104, 104, 104, 112, 40, 32, 80, 88, 120, 72, 32, 32, 72, 80, 64, 72]
+SHARES = [128, 64, 56, 48, 88, 40, 16, 48, 128, 40, 112, 72, 96, 24, 24, 56]
 XQ = 0
-XCAST = [0, 0, 1, 1]
-W2CAST = [1, 0]
-SEQ = "xxxx 300c xxxx P00 301c 100c 101c P10 P01 P11 v0 310c 111a 110c 311a 311b 111b v1"
-QS = [1, 1, 4, 2, 1, 1, 2, 4, 1, 1, 1, 1, 1, 1, 1, 4]
-WB = 5
-BE = [1, 0, 0, 0, 0, 0, 0, 0]
-YE = [0, 0, 0, 1]
-RB = 5
+XCAST = [0, 0, 0, 1]
+W2CAST = [0, 0]
+SEQ = "xxxx xxxx P00 P10 P01 P11 300c 301c 100c 101c v0 310c 311c 110c 111a 111b v1"
+QS = [1, 1, 1, 1, 1, 1, 1, 2, 1, 1, 1, 1, 1, 1, 1, 4]
+LATE = 1
+PARK = 0
+PARKB = 1
+PARKY = 0
+WB = 3
+BE = [0, 0, 0, 0, 0, 0, 0, 0]
+YE = [0, 0, 0, 0]
+RB = 6
 PB = 3
+PBS = [3, 3, 2]
 
 
 def tile_moe_pre_glu_relu_kernel(tc, xT, w1, w3, w2, gate, offs, out):
@@ -44,7 +49,7 @@ def tile_moe_pre_glu_relu_kernel(tc, xT, w1, w3, w2, gate, offs, out):
         stream = ctx.enter_context(tc.tile_pool(name="stream", bufs=RB))
         stage = ctx.enter_context(tc.tile_pool(name="stage", bufs=4))
         psum = ctx.enter_context(tc.psum_pool(name="psum", bufs=PB))
-        psum_y = ctx.enter_context(tc.psum_pool(name="psum_y", bufs=2))
+        psum_y = ctx.enter_context(tc.psum_pool(name="psum_y", bufs=PBS[2]))
 
         offsets = keep.tile([P, E * C // LIST_COLS], U16, name="offsets")
         gate_sb = keep.tile([P, E * C], F32, name="gate_sb")
@@ -55,6 +60,8 @@ def tile_moe_pre_glu_relu_kernel(tc, xT, w1, w3, w2, gate, offs, out):
         w2_mx = {}
         b_sb = {}
         h_mx = {}
+        last_w = {}
+        spent = {}
 
         def quantize(grouped, name, calls=1):
             words = grouped.shape[1] // PACK
@@ -99,6 +106,8 @@ def tile_moe_pre_glu_relu_kernel(tc, xT, w1, w3, w2, gate, offs, out):
             for q in range(first, last):
                 share = SHARES[8 * e + (4 if which == 1 else 0) + 2 * g + q]
                 grouped = stage.tile([P, PASS * PACK], BF16, name="w_grouped", align_bytes=64, bufs=WB)
+                last_w[which, e, g, q] = grouped
+                spent[which, e, g, q] = raw[:, :, (q - first) * PASS : (q - first + 1) * PASS]
                 dst = grouped[:].rearrange("p (t m j) -> p m j t", t=PACK, j=PACK)
                 src = raw[:, :, (q - first) * PASS : (q - first + 1) * PASS].rearrange("p j (m t) -> p m j t", t=PACK)
                 if share > 0:
@@ -121,7 +130,7 @@ def tile_moe_pre_glu_relu_kernel(tc, xT, w1, w3, w2, gate, offs, out):
             w2_mx[e] = quantize(grouped[:], "w2_%d" % e)
 
         def first_layer(which, e, q, s):
-            bank = psum.tile([P, PACK, HALF], F32, name="bank_%d" % which)
+            bank = psum.tile([P, PACK, HALF], F32, name="bank_%d" % which, bufs=PBS[which // 2])
             cols = slice(s * HALF, (s + 1) * HALF)
             for t in range(PACK):
                 for g in range(KP):
@@ -141,18 +150,25 @@ def tile_moe_pre_glu_relu_kernel(tc, xT, w1, w3, w2, gate, offs, out):
         def linear_branch(e, q):
             for s in range(HALVES):
                 sums = first_layer(3, e, q, s)
-                held = stage.tile([P, HALF, PACK], F32, name="b_held")
+                if PARKB:
+                    held = spent[1, e, 0, q][:, s, :].rearrange("p (n t) -> p n t", t=PACK)
+                else:
+                    held = stage.tile([P, HALF, PACK], F32, name="b_held")
                 (nc.vector.tensor_copy if BE[4 * e + 2 * q + s] else nc.scalar.copy)(out=held[:], in_=sums)
                 b_sb[e, q, s] = held
 
         def hidden(e, q):
             for s in range(HALVES):
                 sums = first_layer(1, e, q, s)
-                grouped = stage.tile([P, HALF, PACK], BF16, name="h_grouped", align_bytes=64)
+                if PARK > e and q == 0:
+                    grouped = last_w[1, e, 1, 1][:, s * PASS : (s + 1) * PASS]
+                else:
+                    fresh = stage.tile([P, HALF * PACK], BF16, name="h_grouped", align_bytes=64)
+                    grouped = fresh[:]
                 nc.vector.scalar_tensor_tensor(
-                    out=grouped[:], in0=sums, scalar=0.0, in1=b_sb[e, q, s][:], op0=MAX, op1=MULT
+                    out=grouped.rearrange("p (n t) -> p n t", t=PACK), in0=sums, scalar=0.0, in1=b_sb[e, q, s][:], op0=MAX, op1=MULT
                 )
-                h_mx[e, q, s] = quantize(grouped[:].rearrange("p n t -> p (n t)"), "h_%d_%d_%d" % (e, q, s))
+                h_mx[e, q, s] = quantize(grouped, "h_%d_%d_%d" % (e, q, s))
 
         def second_layer(e):
             w_codes, w_scales = w2_mx[e]
@@ -169,7 +185,10 @@ def tile_moe_pre_glu_relu_kernel(tc, xT, w1, w3, w2, gate, offs, out):
                         start=(q == 0),
                         stop=(q == HP - 1),
                     )
-                y = stage.tile([P, HALF], F32, name="y")
+                if PARKY and e == 0:
+                    y = spent[3, 1, 0, PARKY - 1][:, s, :HALF]
+                else:
+                    y = stage.tile([P, HALF], F32, name="y")
                 (nc.vector.tensor_copy if YE[2 * e + s] else nc.scalar.copy)(out=y[:], in_=bank[:])
                 first = (e * C + s * HALF) // LIST_COLS
                 nc.vector.tensor_copy(out_sb[:].indirect(offsets[:, first : first + HALF // LIST_COLS]), y[:])
@@ -198,16 +217,16 @@ def tile_moe_pre_glu_relu_kernel(tc, xT, w1, w3, w2, gate, offs, out):
                 prepare_w2(item[1], item[2])
             else:
                 prepare_w(item[6], *item[1:6])
-            for e in range(E):
+            for e in range(E if not LATE or item is todo[-1] else 0):
                 ready_x = all((e, g) in x_mx for g in range(KP))
                 for q in range(HP):
-                    if ready_x and ("b", e, q) not in did and all((3, e, g, q) in w_mx for g in range(KP)):
+                    if ready_x and ("b", e, q) not in did and all((3, e, g, q) in w_mx for g in range(KP)) and (not PARKB or (1, e, 0, q) in w_mx):
                         did.add(("b", e, q))
                         linear_branch(e, q)
-                    if ("b", e, q) in did and ("h", e, q) not in did and all((1, e, g, q) in w_mx for g in range(KP)):
+                    if ("b", e, q) in did and ("h", e, q) not in did and all((1, e, g, q) in w_mx for g in range(KP)) and (PARK <= e or (1, e, 1, 1) in w_mx):
                         did.add(("h", e, q))
                         hidden(e, q)
-                if ("y", e) not in did and e in w2_mx and all(("h", e, q) in did for q in range(HP)):
+                if ("y", e) not in did and e in w2_mx and all(("h", e, q) in did for q in range(HP)) and (not PARKY or (3, 1, 0, PARKY - 1) in w_mx):
                     did.add(("y", e))
                     second_layer(e)
         nc.sync.dma_start(out=out, in_=out_sb[:])

@@ -1,10 +1,11 @@
 from contextlib import ExitStack
 
 import concourse.mybir as mybir
+from concourse.masks import make_identity
 
 K, T, E, C, H, N = 1024, 512, 2, 256, 1024, 128
 FLOPS = 2 * E * C * (2 * K * H + H * N)
-BYTES = 4 * (K * T + 2 * E * K * H + E * H * N + 128 * T + N * T) + 2 * 128 * 32
+BYTES = 4 * (K * T + 2 * E * K * H + E * H * N + T + N * T) + 2 * 128 * 32
 
 F32 = mybir.dt.float32
 BF16 = mybir.dt.bfloat16
@@ -24,44 +25,35 @@ HALF = 128
 HALVES = C // HALF
 LIST_COLS = 16
 
-SHARES = [128, 64, 56, 48, 88, 40, 16, 48, 128, 40, 112, 72, 96, 24, 24, 56]
-XQ = 0
-XCAST = [0, 0, 0, 1]
-W2CAST = [0, 0]
-SEQ = "xxxx xxxx P00 P10 P01 P11 300c 301c 100c 101c v0 310c 311c 110c 111a 111b v1"
-QS = [1, 1, 1, 1, 1, 1, 1, 2, 1, 1, 1, 1, 1, 1, 1, 4]
-LATE = 1
-PARK = 0
-PARKB = 1
-PARKY = 0
-WB = 3
-BE = [0, 0, 0, 0, 0, 0, 0, 0]
-YE = [0, 0, 0, 0]
-RB = 6
-PB = 3
-PBS = [3, 3, 2]
+SHARE_ALL = 128
+SHARE_CATCH = 96
+SHARE_MOST = 96
+SHARE_EVEN = 44
+SHARE_W5 = 80
 
 
 def tile_moe_pre_glu_relu_kernel(tc, xT, w1, w3, w2, gate, offs, out):
     nc = tc.nc
     with ExitStack() as ctx:
         keep = ctx.enter_context(tc.tile_pool(name="keep", bufs=1))
-        stream = ctx.enter_context(tc.tile_pool(name="stream", bufs=RB))
+        stream = ctx.enter_context(tc.tile_pool(name="stream", bufs=6))
         stage = ctx.enter_context(tc.tile_pool(name="stage", bufs=4))
-        psum = ctx.enter_context(tc.psum_pool(name="psum", bufs=PB))
-        psum_y = ctx.enter_context(tc.psum_pool(name="psum_y", bufs=PBS[2]))
+        psum = ctx.enter_context(tc.psum_pool(name="psum", bufs=6))
+        psum_y = ctx.enter_context(tc.psum_pool(name="psum_y", bufs=2))
 
         offsets = keep.tile([P, E * C // LIST_COLS], U16, name="offsets")
         gate_sb = keep.tile([P, E * C], F32, name="gate_sb")
         out_sb = keep.tile([P, T], F32, name="out_sb")
         x_rows = {}
         x_mx = {}
+        w_raw = {}
+        w_grouped = {}
         w_mx = {}
+        w2_raw = {}
         w2_mx = {}
         b_sb = {}
+        h_grouped = {}
         h_mx = {}
-        last_w = {}
-        spent = {}
 
         def quantize(grouped, name, calls=1):
             words = grouped.shape[1] // PACK
@@ -76,61 +68,61 @@ def tile_moe_pre_glu_relu_kernel(tc, xT, w1, w3, w2, gate, offs, out):
                 )
             return codes, scales
 
-        def load_x(g, j):
-            rows = keep.tile([P, T], F32, name="x_rows_%d_%d" % (g, j))
+        def load_x(g):
             src = xT[g * PASS : (g + 1) * PASS, :].rearrange("(p j) n -> p j n", j=PACK)
-            (nc.scalar if XQ else nc.sync).dma_start(out=rows[:], in_=src[:, j, :])
-            x_rows[g, j] = rows
+            for j in range(PACK):
+                rows = keep.tile([P, T], F32, name="x_rows_%d_%d" % (g, j))
+                nc.sync.dma_start(out=rows[:], in_=src[:, j, :])
+                x_rows[g, j] = rows
 
         def prepare_x(e, g):
             slots = slice(e * C, (e + 1) * C)
             entries = offsets[:, e * C // LIST_COLS : (e + 1) * C // LIST_COLS]
-            picked = stage.tile([P, PACK, C], F32, name="picked", bufs=2)
+            picked = stage.tile([P, PACK, C], F32, name="picked", bufs=4)
             for j in range(PACK):
                 nc.vector.tensor_tensor(picked[:, j, :], x_rows[g, j][:].indirect(entries), gate_sb[:, slots], MULT)
             grouped = stage.tile([P, C * PACK], BF16, name="x_grouped", align_bytes=64, bufs=2)
-            (nc.vector.tensor_copy if XCAST[2 * e + g] else nc.scalar.copy)(
+            (nc.scalar.copy if g == 0 else nc.vector.tensor_copy)(
                 out=grouped[:].rearrange("p (c i j) -> p c j i", i=4, j=PACK),
                 in_=picked[:].rearrange("p j (c i) -> p c j i", i=4),
             )
             x_mx[e, g] = quantize(grouped[:], "x_%d_%d" % (e, g))
 
-        def load_w(w, e, g, first, last):
+        def load_w(which, e, g, first=0, last=HP):
             cols = slice(first * PASS, last * PASS)
-            raw = stream.tile([P, PACK, (last - first) * PASS], F32, name="raw")
+            raw = stream.tile([P, PACK, (last - first) * PASS], F32, name="raw", align_bytes=64)
+            w = w1 if which == 1 else w3
             src = w[e, g * PASS : (g + 1) * PASS, :].rearrange("(p j) c -> p j c", j=PACK)
             nc.sync.dma_start(out=raw[:], in_=src[:, :, cols])
-            return raw
-
-        def prepare_w(raw, which, e, g, first, last):
             for q in range(first, last):
-                share = SHARES[8 * e + (4 if which == 1 else 0) + 2 * g + q]
-                grouped = stage.tile([P, PASS * PACK], BF16, name="w_grouped", align_bytes=64, bufs=WB)
-                last_w[which, e, g, q] = grouped
-                spent[which, e, g, q] = raw[:, :, (q - first) * PASS : (q - first + 1) * PASS]
-                dst = grouped[:].rearrange("p (t m j) -> p m j t", t=PACK, j=PACK)
-                src = raw[:, :, (q - first) * PASS : (q - first + 1) * PASS].rearrange("p j (m t) -> p m j t", t=PACK)
-                if share > 0:
-                    nc.scalar.copy(out=dst[:, :share], in_=src[:, :share])
-                if share < P:
-                    nc.vector.tensor_copy(out=dst[:, share:], in_=src[:, share:])
-                w_mx[which, e, g, q] = quantize(grouped[:], "w%d_%d_%d_%d" % (which, e, g, q), QS[8 * e + (4 if which == 1 else 0) + 2 * g + q])
+                w_raw[which, e, g, q] = raw[:, :, (q - first) * PASS : (q - first + 1) * PASS]
+
+        def prepare_w(which, e, g, q, share, calls=1):
+            grouped = stage.tile([P, PASS * PACK], BF16, name="w_grouped", align_bytes=64, bufs=4)
+            dst = grouped[:].rearrange("p (t m j) -> p m j t", t=PACK, j=PACK)
+            src = w_raw[which, e, g, q].rearrange("p j (m t) -> p m j t", t=PACK)
+            if share > 0:
+                nc.scalar.copy(out=dst[:, :share], in_=src[:, :share])
+            if share < P:
+                nc.vector.tensor_copy(out=dst[:, share:], in_=src[:, share:])
+            w_grouped[which, e, g, q] = grouped
+            w_mx[which, e, g, q] = quantize(grouped[:], "w%d_%d_%d_%d" % (which, e, g, q), calls)
 
         def load_w2(e):
-            raw = stream.tile([P, HP, PACK * N], F32, name="raw")
+            raw = stream.tile([P, HP, PACK * N], F32, name="raw", align_bytes=64)
             nc.sync.dma_start(out=raw[:], in_=w2[e].rearrange("(q p j) n -> p q (j n)", p=P, j=PACK))
-            return raw
+            w2_raw[e] = raw
 
-        def prepare_w2(e, raw):
+        def prepare_w2(e):
             grouped = stage.tile([P, HP * N * PACK], BF16, name="w2_grouped", align_bytes=64, bufs=2)
-            (nc.vector.tensor_copy if W2CAST[e] else nc.scalar.copy)(
+            nc.scalar.copy(
                 out=grouped[:].rearrange("p (q c i j) -> p q c j i", q=HP, i=4, j=PACK),
-                in_=raw[:].rearrange("p q (j c i) -> p q c j i", j=PACK, i=4),
+                in_=w2_raw[e][:].rearrange("p q (j c i) -> p q c j i", j=PACK, i=4),
             )
             w2_mx[e] = quantize(grouped[:], "w2_%d" % e)
 
         def first_layer(which, e, q, s):
-            bank = psum.tile([P, PACK, HALF], F32, name="bank_%d" % which, bufs=PBS[which // 2])
+            bank = psum.tile([P, PACK, HALF], F32, name="bank_%d" % which, bufs=3)
             cols = slice(s * HALF, (s + 1) * HALF)
             for t in range(PACK):
                 for g in range(KP):
@@ -147,86 +139,109 @@ def tile_moe_pre_glu_relu_kernel(tc, xT, w1, w3, w2, gate, offs, out):
                     )
             return bank[:].rearrange("p t n -> p n t")
 
-        def linear_branch(e, q):
-            for s in range(HALVES):
-                sums = first_layer(3, e, q, s)
-                if PARKB:
-                    held = spent[1, e, 0, q][:, s, :].rearrange("p (n t) -> p n t", t=PACK)
-                else:
-                    held = stage.tile([P, HALF, PACK], F32, name="b_held")
-                (nc.vector.tensor_copy if BE[4 * e + 2 * q + s] else nc.scalar.copy)(out=held[:], in_=sums)
-                b_sb[e, q, s] = held
+        def linear_branch(e, q, s, spent):
+            sums = first_layer(3, e, q, s)
+            held = spent[:, s, :].rearrange("p (n t) -> p n t", t=PACK)
+            nc.scalar.copy(out=held, in_=sums)
+            b_sb[e, q, s] = held
 
-        def hidden(e, q):
-            for s in range(HALVES):
-                sums = first_layer(1, e, q, s)
-                if PARK > e and q == 0:
-                    grouped = last_w[1, e, 1, 1][:, s * PASS : (s + 1) * PASS]
-                else:
-                    fresh = stage.tile([P, HALF * PACK], BF16, name="h_grouped", align_bytes=64)
-                    grouped = fresh[:]
-                nc.vector.scalar_tensor_tensor(
-                    out=grouped.rearrange("p (n t) -> p n t", t=PACK), in0=sums, scalar=0.0, in1=b_sb[e, q, s][:], op0=MAX, op1=MULT
-                )
-                h_mx[e, q, s] = quantize(grouped, "h_%d_%d_%d" % (e, q, s))
+        def hidden(e, q, s, spent=None):
+            sums = first_layer(1, e, q, s)
+            if spent is None:
+                fresh = stage.tile([P, HALF * PACK], BF16, name="h_grouped", align_bytes=64)
+                grouped = fresh[:]
+            else:
+                grouped = spent
+            nc.vector.scalar_tensor_tensor(
+                out=grouped.rearrange("p (n t) -> p n t", t=PACK), in0=sums, scalar=0.0, in1=b_sb[e, q, s], op0=MAX, op1=MULT
+            )
+            h_grouped[e, q, s] = grouped
 
-        def second_layer(e):
+        def quantize_hidden(e, q, s):
+            h_mx[e, q, s] = quantize(h_grouped[e, q, s], "h_%d_%d_%d" % (e, q, s))
+
+        def second_layer(e, s, y):
             w_codes, w_scales = w2_mx[e]
+            bank = psum_y.tile([P, HALF], F32, name="bank_y")
+            for q in range(HP):
+                h_codes, h_scales = h_mx[e, q, s]
+                nc.tensor.matmul_mx(
+                    out=bank[:],
+                    lhsT=w_codes[:, q * N : (q + 1) * N].bitcast(FP8X4),
+                    lhsT_scale=w_scales[:, q * N : (q + 1) * N],
+                    rhs=h_codes[:].bitcast(FP8X4),
+                    rhs_scale=h_scales[:],
+                    start=(q == 0),
+                    stop=(q == HP - 1),
+                )
+            nc.scalar.copy(out=y[:, s * HALF : (s + 1) * HALF], in_=bank[:])
+
+        def put_back(e, y, first, count):
+            column = (e * C + first) // LIST_COLS
+            entries = offsets[:, column : column + count // LIST_COLS]
+            nc.vector.tensor_copy(out_sb[:].indirect(entries), y[:, first : first + count])
+
+        def finish(e, y, count):
             for s in range(HALVES):
-                bank = psum_y.tile([P, HALF], F32, name="bank_y")
-                for q in range(HP):
-                    h_codes, h_scales = h_mx[e, q, s]
-                    nc.tensor.matmul_mx(
-                        out=bank[:],
-                        lhsT=w_codes[:, q * N : (q + 1) * N].bitcast(FP8X4),
-                        lhsT_scale=w_scales[:, q * N : (q + 1) * N],
-                        rhs=h_codes[:].bitcast(FP8X4),
-                        rhs_scale=h_scales[:],
-                        start=(q == 0),
-                        stop=(q == HP - 1),
-                    )
-                if PARKY and e == 0:
-                    y = spent[3, 1, 0, PARKY - 1][:, s, :HALF]
-                else:
-                    y = stage.tile([P, HALF], F32, name="y")
-                (nc.vector.tensor_copy if YE[2 * e + s] else nc.scalar.copy)(out=y[:], in_=bank[:])
-                first = (e * C + s * HALF) // LIST_COLS
-                nc.vector.tensor_copy(out_sb[:].indirect(offsets[:, first : first + HALF // LIST_COLS]), y[:])
+                second_layer(e, s, y)
+            for first in range(0, C, count):
+                put_back(e, y, first, count)
 
         nc.sync.dma_start(offsets[:], offs)
-        (nc.scalar if XQ else nc.sync).dma_start(out=gate_sb[:], in_=gate[:P, :])
-        planes = [(g, j) for g in range(KP) for j in range(PACK)]
-        todo = []
-        for tok in SEQ.split():
-            if tok[0] == "x":
-                for r in range(len(tok)):
-                    load_x(*planes.pop(0))
-            elif tok[0] == "P":
-                todo.append(("P", int(tok[1]), int(tok[2])))
-            elif tok[0] == "v":
-                todo.append(("v", int(tok[1]), load_w2(int(tok[1]))))
+        gate_row = keep.tile([P, PACK], F32, name="gate_row")
+        nc.sync.dma_start(out=gate_row[:], in_=gate[0].rearrange("(p t) -> p t", t=PACK))
+        identity = keep.tile([P, P], F32, name="identity")
+        make_identity(nc, identity[:])
+        spread = psum.tile([P, PACK, P], F32, name="bank_1", bufs=3)
+        for t in range(PACK):
+            nc.tensor.transpose(spread[:, t, :], gate_row[:, t : t + 1].to_broadcast([P, P]), identity[:])
+        nc.scalar.copy(out=gate_sb[:].rearrange("p (n t) -> p n t", t=PACK), in_=spread[:].rearrange("p t n -> p n t"))
+        for g in range(KP):
+            load_x(g)
+        for g in range(KP):
+            for e in range(E):
+                prepare_x(e, g)
+        for e in range(E):
+            last_expert = e == E - 1
+            load_w(3, e, 0)
+            load_w(3, e, 1)
+            load_w(1, e, 0)
+            if last_expert:
+                load_w(1, e, 1, 0, 1)
+                load_w(1, e, 1, 1, 2)
             else:
-                which, e, g = int(tok[0]), int(tok[1]), int(tok[2])
-                first, last = {"a": (0, 1), "b": (1, 2), "c": (0, 2)}[tok[3]]
-                todo.append(("w", which, e, g, first, last, load_w(w1 if which == 1 else w3, e, g, first, last)))
-        did = set()
-        for item in todo:
-            if item[0] == "P":
-                prepare_x(item[1], item[2])
-            elif item[0] == "v":
-                prepare_w2(item[1], item[2])
+                load_w(1, e, 1)
+            load_w2(e)
+
+            prepare_w(3, e, 0, 0, SHARE_ALL if e == 0 else SHARE_MOST)
+            if e > 0:
+                finish(e - 1, w_raw[3, e, 0, 0][:, 0, :C], C)
+            prepare_w(3, e, 0, 1, SHARE_ALL if e == 0 else SHARE_MOST)
+            for q in range(HP):
+                prepare_w(3, e, 1, q, SHARE_CATCH if e == 0 else SHARE_W5)
+            for q in range(HP):
+                prepare_w(1, e, 0, q, SHARE_EVEN)
+            for q in range(1 if last_expert else HP):
+                for s in range(HALVES):
+                    linear_branch(e, q, s, w_raw[1, e, 0, q])
+            prepare_w(1, e, 1, 0, SHARE_EVEN)
+            prepare_w(1, e, 1, 1, SHARE_EVEN, PACK if last_expert else 1)
+            if last_expert:
+                linear_branch(e, 1, 0, w_raw[1, e, 1, 1])
+                prepare_w2(e)
+                linear_branch(e, 1, 1, w_raw[1, e, 1, 1])
+                for s in range(HALVES):
+                    hidden(e, 0, s, w_grouped[1, e, 1, 1][:, (PACK - HALVES + s) * PASS : (PACK - HALVES + s + 1) * PASS])
             else:
-                prepare_w(item[6], *item[1:6])
-            for e in range(E if not LATE or item is todo[-1] else 0):
-                ready_x = all((e, g) in x_mx for g in range(KP))
-                for q in range(HP):
-                    if ready_x and ("b", e, q) not in did and all((3, e, g, q) in w_mx for g in range(KP)) and (not PARKB or (1, e, 0, q) in w_mx):
-                        did.add(("b", e, q))
-                        linear_branch(e, q)
-                    if ("b", e, q) in did and ("h", e, q) not in did and all((1, e, g, q) in w_mx for g in range(KP)) and (PARK <= e or (1, e, 1, 1) in w_mx):
-                        did.add(("h", e, q))
-                        hidden(e, q)
-                if ("y", e) not in did and e in w2_mx and all(("h", e, q) in did for q in range(HP)) and (not PARKY or (3, 1, 0, PARKY - 1) in w_mx):
-                    did.add(("y", e))
-                    second_layer(e)
+                prepare_w2(e)
+                for s in range(HALVES):
+                    hidden(e, 0, s)
+            hidden(e, 1, 0)
+            for s in range(HALVES):
+                quantize_hidden(e, 0, s)
+            quantize_hidden(e, 1, 0)
+            hidden(e, 1, 1)
+            quantize_hidden(e, 1, 1)
+        last_y = keep.tile([P, C], F32, name="last_y")
+        finish(E - 1, last_y[:], HALF)
         nc.sync.dma_start(out=out, in_=out_sb[:])

@@ -26,7 +26,8 @@ HALVES = C // HALF
 LIST_COLS = 16
 
 SHARE_ALL = 128
-SHARE_CATCH = 96
+SHARE_CATCH = 128
+SHARE_W2 = 64
 SHARE_MOST = 96
 SHARE_EVEN = 44
 SHARE_W5 = 80
@@ -69,22 +70,23 @@ def tile_moe_pre_glu_relu_kernel(tc, xT, w1, w3, w2, gate, offs, out):
             return codes, scales
 
         def load_x(g):
-            src = xT[g * PASS : (g + 1) * PASS, :].rearrange("(p j) n -> p j n", j=PACK)
-            for j in range(PACK):
-                rows = keep.tile([P, T], F32, name="x_rows_%d_%d" % (g, j))
-                nc.sync.dma_start(out=rows[:], in_=src[:, j, :])
-                x_rows[g, j] = rows
+            rows = keep.tile([P, PACK * T], F32, name="x_rows_%d" % g)
+            src = xT[g * PASS : (g + 1) * PASS, :].rearrange("(p j) n -> p (j n)", j=PACK)
+            nc.sync.dma_start(out=rows[:], in_=src)
+            x_rows[g] = rows
 
         def prepare_x(e, g):
-            slots = slice(e * C, (e + 1) * C)
             entries = offsets[:, e * C // LIST_COLS : (e + 1) * C // LIST_COLS]
-            picked = stage.tile([P, PACK, C], F32, name="picked", bufs=4)
+            picked = stage.tile([P, PACK, C], F32, name="picked", bufs=2)
             for j in range(PACK):
-                nc.vector.tensor_tensor(picked[:, j, :], x_rows[g, j][:].indirect(entries), gate_sb[:, slots], MULT)
+                nc.vector.tensor_copy(picked[:, j, :], x_rows[g][:, j * T : (j + 1) * T].indirect(entries))
             grouped = stage.tile([P, C * PACK], BF16, name="x_grouped", align_bytes=64, bufs=2)
-            (nc.scalar.copy if g == 0 else nc.vector.tensor_copy)(
-                out=grouped[:].rearrange("p (c i j) -> p c j i", i=4, j=PACK),
-                in_=picked[:].rearrange("p j (c i) -> p c j i", i=4),
+            weights = gate_sb[:, e * C : (e + 1) * C].rearrange("p (c i) -> p c i", i=2)
+            nc.vector.tensor_tensor(
+                grouped[:].rearrange("p (c i j) -> p c j i", i=2, j=PACK),
+                picked[:].rearrange("p j (c i) -> p c j i", i=2),
+                weights.unsqueeze(2).to_broadcast([P, C // 2, PACK, 2]),
+                MULT,
             )
             x_mx[e, g] = quantize(grouped[:], "x_%d_%d" % (e, g))
 
@@ -187,6 +189,7 @@ def tile_moe_pre_glu_relu_kernel(tc, xT, w1, w3, w2, gate, offs, out):
             for first in range(0, C, count):
                 put_back(e, y, first, count)
 
+        load_x(0)
         nc.sync.dma_start(offsets[:], offs)
         gate_row = keep.tile([P, PACK], F32, name="gate_row")
         nc.sync.dma_start(out=gate_row[:], in_=gate[0].rearrange("(p t) -> p t", t=PACK))
@@ -196,14 +199,15 @@ def tile_moe_pre_glu_relu_kernel(tc, xT, w1, w3, w2, gate, offs, out):
         for t in range(PACK):
             nc.tensor.transpose(spread[:, t, :], gate_row[:, t : t + 1].to_broadcast([P, P]), identity[:])
         nc.scalar.copy(out=gate_sb[:].rearrange("p (n t) -> p n t", t=PACK), in_=spread[:].rearrange("p t n -> p n t"))
-        for g in range(KP):
-            load_x(g)
+        load_w(3, 0, 0)
+        load_x(1)
         for g in range(KP):
             for e in range(E):
                 prepare_x(e, g)
         for e in range(E):
             last_expert = e == E - 1
-            load_w(3, e, 0)
+            if e > 0:
+                load_w(3, e, 0)
             load_w(3, e, 1)
             load_w(1, e, 0)
             if last_expert:
@@ -220,7 +224,7 @@ def tile_moe_pre_glu_relu_kernel(tc, xT, w1, w3, w2, gate, offs, out):
             for q in range(HP):
                 prepare_w(3, e, 1, q, SHARE_CATCH if e == 0 else SHARE_W5)
             for q in range(HP):
-                prepare_w(1, e, 0, q, SHARE_EVEN)
+                prepare_w(1, e, 0, q, SHARE_EVEN if last_expert else SHARE_W2)
             for q in range(1 if last_expert else HP):
                 for s in range(HALVES):
                     linear_branch(e, q, s, w_raw[1, e, 0, q])

@@ -28,6 +28,7 @@ LIST_COLS = 16
 SHARE_ALL = 128
 SHARE_CATCH = 128
 SHARE_W2 = 64
+SHARE_LAST = 56
 SHARE_MOST = 96
 SHARE_EVEN = 44
 SHARE_W5 = 80
@@ -99,7 +100,7 @@ def tile_moe_pre_glu_relu_kernel(tc, xT, w1, w3, w2, gate, offs, out):
             for q in range(first, last):
                 w_raw[which, e, g, q] = raw[:, :, (q - first) * PASS : (q - first + 1) * PASS]
 
-        def prepare_w(which, e, g, q, share, calls=1):
+        def cast_w(which, e, g, q, share):
             grouped = stage.tile([P, PASS * PACK], BF16, name="w_grouped", align_bytes=64, bufs=4)
             dst = grouped[:].rearrange("p (t m j) -> p m j t", t=PACK, j=PACK)
             src = w_raw[which, e, g, q].rearrange("p j (m t) -> p m j t", t=PACK)
@@ -108,7 +109,13 @@ def tile_moe_pre_glu_relu_kernel(tc, xT, w1, w3, w2, gate, offs, out):
             if share < P:
                 nc.vector.tensor_copy(out=dst[:, share:], in_=src[:, share:])
             w_grouped[which, e, g, q] = grouped
-            w_mx[which, e, g, q] = quantize(grouped[:], "w%d_%d_%d_%d" % (which, e, g, q), calls)
+
+        def quantize_w(which, e, g, q, calls=1):
+            w_mx[which, e, g, q] = quantize(w_grouped[which, e, g, q][:], "w%d_%d_%d_%d" % (which, e, g, q), calls)
+
+        def prepare_w(which, e, g, q, share):
+            cast_w(which, e, g, q, share)
+            quantize_w(which, e, g, q)
 
         def load_w2(e):
             raw = stream.tile([P, HP, PACK * N], F32, name="raw", align_bytes=64)
@@ -229,23 +236,25 @@ def tile_moe_pre_glu_relu_kernel(tc, xT, w1, w3, w2, gate, offs, out):
                 for s in range(HALVES):
                     linear_branch(e, q, s, w_raw[1, e, 0, q])
             prepare_w(1, e, 1, 0, SHARE_EVEN)
-            prepare_w(1, e, 1, 1, SHARE_EVEN, PACK if last_expert else 1)
             if last_expert:
+                cast_w(1, e, 1, 1, SHARE_LAST)
+                hidden(e, 0, 0, w_raw[1, e, 1, 1][:, PACK - 1, PASS // 2 :].bitcast(BF16))
+                quantize_w(1, e, 1, 1, PACK)
                 linear_branch(e, 1, 0, w_raw[1, e, 1, 1])
                 prepare_w2(e)
                 linear_branch(e, 1, 1, w_raw[1, e, 1, 1])
-                for s in range(HALVES):
-                    hidden(e, 0, s, w_grouped[1, e, 1, 1][:, (PACK - HALVES + s) * PASS : (PACK - HALVES + s + 1) * PASS])
+                hidden(e, 0, 1, w_grouped[1, e, 1, 1][:, (PACK - 1) * PASS :])
             else:
+                prepare_w(1, e, 1, 1, SHARE_EVEN)
                 prepare_w2(e)
                 for s in range(HALVES):
                     hidden(e, 0, s)
             hidden(e, 1, 0)
-            for s in range(HALVES):
-                quantize_hidden(e, 0, s)
-            quantize_hidden(e, 1, 0)
+            for q in range(HP):
+                quantize_hidden(e, q, 0)
             hidden(e, 1, 1)
-            quantize_hidden(e, 1, 1)
+            for q in range(HP):
+                quantize_hidden(e, q, 1)
         last_y = keep.tile([P, C], F32, name="last_y")
         finish(E - 1, last_y[:], HALF)
         nc.sync.dma_start(out=out, in_=out_sb[:])

@@ -5,7 +5,7 @@ from concourse.masks import make_identity
 
 K, T, E, C, H, N = 1024, 512, 2, 256, 1024, 128
 FLOPS = 2 * E * C * (2 * K * H + H * N)
-BYTES = 4 * (K * T + 2 * E * K * H + E * H * N + T + N * T) + 2 * 128 * 32
+BYTES = 4 * (K * T + 2 * E * K * H + E * H * N + E * C + N * T) + 2 * 128 * 32
 
 F32 = mybir.dt.float32
 BF16 = mybir.dt.bfloat16
@@ -23,29 +23,34 @@ KP = K // PASS
 HP = H // PASS
 HALF = 128
 HALVES = C // HALF
-LIST_COLS = 16
+PER_COLUMN = 16
+RELU, LINEAR = 1, 3
 
-SHARE_ALL = 128
-SHARE_CATCH = 128
-SHARE_W2 = 64
-SHARE_LAST = 56
-SHARE_MOST = 96
+SHARE_GATHERING = 128
+SHARE_CATCHING_UP = 112
+SHARE_HIDDEN = 96
+SHARE_SCATTERING = 80
 SHARE_EVEN = 44
-SHARE_W5 = 80
+SHARE_LAST = 56
+
+RAW_BUFS = 6
+CAST_BUFS = 6
+BRANCH_BANKS = 3
 
 
 def tile_moe_pre_glu_relu_kernel(tc, xT, w1, w3, w2, gate, offs, out):
     nc = tc.nc
     with ExitStack() as ctx:
         keep = ctx.enter_context(tc.tile_pool(name="keep", bufs=1))
-        stream = ctx.enter_context(tc.tile_pool(name="stream", bufs=6))
-        stage = ctx.enter_context(tc.tile_pool(name="stage", bufs=4))
-        psum = ctx.enter_context(tc.psum_pool(name="psum", bufs=6))
-        psum_y = ctx.enter_context(tc.psum_pool(name="psum_y", bufs=2))
+        stream = ctx.enter_context(tc.tile_pool(name="stream", bufs=RAW_BUFS))
+        stage = ctx.enter_context(tc.tile_pool(name="stage", bufs=HP * HALVES))
+        psum = ctx.enter_context(tc.psum_pool(name="psum", bufs=BRANCH_BANKS))
+        psum_y = ctx.enter_context(tc.psum_pool(name="psum_y", bufs=HALVES))
 
-        offsets = keep.tile([P, E * C // LIST_COLS], U16, name="offsets")
+        offsets = keep.tile([P, E * C // PER_COLUMN], U16, name="offsets")
         gate_sb = keep.tile([P, E * C], F32, name="gate_sb")
         out_sb = keep.tile([P, T], F32, name="out_sb")
+        last_y = keep.tile([P, C], F32, name="last_y")
         x_rows = {}
         x_mx = {}
         w_raw = {}
@@ -70,52 +75,63 @@ def tile_moe_pre_glu_relu_kernel(tc, xT, w1, w3, w2, gate, offs, out):
                 )
             return codes, scales
 
+        def entries(first, count):
+            return offsets[:, first // PER_COLUMN : (first + count) // PER_COLUMN]
+
+        def spread_gate():
+            gate_row = keep.tile([P, PACK], F32, name="gate_row")
+            nc.sync.dma_start(out=gate_row[:], in_=gate[0].rearrange("(p t) -> p t", t=PACK))
+            identity = keep.tile([P, P], F32, name="identity")
+            make_identity(nc, identity[:])
+            spread = psum.tile([P, PACK, P], F32, name="bank_%d" % RELU)
+            for t in range(PACK):
+                nc.tensor.transpose(spread[:, t, :], gate_row[:, t : t + 1].to_broadcast([P, P]), identity[:])
+            nc.scalar.copy(out=gate_sb[:].rearrange("p (n t) -> p n t", t=PACK), in_=spread[:].rearrange("p t n -> p n t"))
+
         def load_x(g):
             rows = keep.tile([P, PACK * T], F32, name="x_rows_%d" % g)
-            src = xT[g * PASS : (g + 1) * PASS, :].rearrange("(p j) n -> p (j n)", j=PACK)
-            nc.sync.dma_start(out=rows[:], in_=src)
+            nc.sync.dma_start(out=rows[:], in_=xT[g * PASS : (g + 1) * PASS, :].rearrange("(p j) n -> p (j n)", j=PACK))
             x_rows[g] = rows
 
-        def prepare_x(e, g):
-            entries = offsets[:, e * C // LIST_COLS : (e + 1) * C // LIST_COLS]
-            picked = stage.tile([P, PACK, C], F32, name="picked", bufs=2)
+        def prepare_x(g):
+            picked = stage.tile([P, PACK, E * C], F32, name="picked", bufs=1)
             for j in range(PACK):
-                nc.vector.tensor_copy(picked[:, j, :], x_rows[g][:, j * T : (j + 1) * T].indirect(entries))
-            grouped = stage.tile([P, C * PACK], BF16, name="x_grouped", align_bytes=64, bufs=2)
-            weights = gate_sb[:, e * C : (e + 1) * C].rearrange("p (c i) -> p c i", i=2)
+                window = x_rows[g][:, j * T : (j + 1) * T]
+                for e in range(E):
+                    nc.vector.tensor_copy(picked[:, j, e * C : (e + 1) * C], window.indirect(entries(e * C, C)))
+            grouped = stage.tile([P, E * C * PACK], BF16, name="grouped", align_bytes=64, bufs=CAST_BUFS)
+            gate_pairs = gate_sb[:].rearrange("p (c i) -> p c i", i=2)
             nc.vector.tensor_tensor(
                 grouped[:].rearrange("p (c i j) -> p c j i", i=2, j=PACK),
                 picked[:].rearrange("p j (c i) -> p c j i", i=2),
-                weights.unsqueeze(2).to_broadcast([P, C // 2, PACK, 2]),
+                gate_pairs.unsqueeze(2).to_broadcast([P, E * C // 2, PACK, 2]),
                 MULT,
             )
-            x_mx[e, g] = quantize(grouped[:], "x_%d_%d" % (e, g))
+            x_mx[g] = quantize(grouped[:], "x_%d" % g)
 
-        def load_w(which, e, g, first=0, last=HP):
-            cols = slice(first * PASS, last * PASS)
+        def load_w(branch, e, g, first=0, last=HP):
             raw = stream.tile([P, PACK, (last - first) * PASS], F32, name="raw", align_bytes=64)
-            w = w1 if which == 1 else w3
-            src = w[e, g * PASS : (g + 1) * PASS, :].rearrange("(p j) c -> p j c", j=PACK)
-            nc.sync.dma_start(out=raw[:], in_=src[:, :, cols])
+            w = w1 if branch == RELU else w3
+            rows = w[e, g * PASS : (g + 1) * PASS, :].rearrange("(p j) c -> p j c", j=PACK)
+            nc.sync.dma_start(out=raw[:], in_=rows[:, :, first * PASS : last * PASS])
             for q in range(first, last):
-                w_raw[which, e, g, q] = raw[:, :, (q - first) * PASS : (q - first + 1) * PASS]
+                w_raw[branch, e, g, q] = raw[:, :, (q - first) * PASS : (q - first + 1) * PASS]
 
-        def cast_w(which, e, g, q, share):
-            grouped = stage.tile([P, PASS * PACK], BF16, name="w_grouped", align_bytes=64, bufs=4)
+        def cast_w(branch, e, g, q, share):
+            grouped = stage.tile([P, PASS * PACK], BF16, name="grouped", align_bytes=64, bufs=CAST_BUFS)
             dst = grouped[:].rearrange("p (t m j) -> p m j t", t=PACK, j=PACK)
-            src = w_raw[which, e, g, q].rearrange("p j (m t) -> p m j t", t=PACK)
-            if share > 0:
-                nc.scalar.copy(out=dst[:, :share], in_=src[:, :share])
+            src = w_raw[branch, e, g, q].rearrange("p j (m t) -> p m j t", t=PACK)
+            nc.scalar.copy(out=dst[:, :share], in_=src[:, :share])
             if share < P:
                 nc.vector.tensor_copy(out=dst[:, share:], in_=src[:, share:])
-            w_grouped[which, e, g, q] = grouped
+            w_grouped[branch, e, g, q] = grouped
 
-        def quantize_w(which, e, g, q, calls=1):
-            w_mx[which, e, g, q] = quantize(w_grouped[which, e, g, q][:], "w%d_%d_%d_%d" % (which, e, g, q), calls)
+        def quantize_w(branch, e, g, q, calls=1):
+            w_mx[branch, e, g, q] = quantize(w_grouped[branch, e, g, q][:], "w%d_%d_%d_%d" % (branch, e, g, q), calls)
 
-        def prepare_w(which, e, g, q, share):
-            cast_w(which, e, g, q, share)
-            quantize_w(which, e, g, q)
+        def prepare_w(branch, e, g, q, share):
+            cast_w(branch, e, g, q, share)
+            quantize_w(branch, e, g, q)
 
         def load_w2(e):
             raw = stream.tile([P, HP, PACK * N], F32, name="raw", align_bytes=64)
@@ -123,39 +139,39 @@ def tile_moe_pre_glu_relu_kernel(tc, xT, w1, w3, w2, gate, offs, out):
             w2_raw[e] = raw
 
         def prepare_w2(e):
-            grouped = stage.tile([P, HP * N * PACK], BF16, name="w2_grouped", align_bytes=64, bufs=2)
+            grouped = stage.tile([P, HP * N * PACK], BF16, name="w2_grouped", align_bytes=64, bufs=E)
             nc.scalar.copy(
                 out=grouped[:].rearrange("p (q c i j) -> p q c j i", q=HP, i=4, j=PACK),
                 in_=w2_raw[e][:].rearrange("p q (j c i) -> p q c j i", j=PACK, i=4),
             )
             w2_mx[e] = quantize(grouped[:], "w2_%d" % e)
 
-        def first_layer(which, e, q, s):
-            bank = psum.tile([P, PACK, HALF], F32, name="bank_%d" % which, bufs=3)
-            cols = slice(s * HALF, (s + 1) * HALF)
+        def first_layer(branch, e, q, s):
+            bank = psum.tile([P, PACK, HALF], F32, name="bank_%d" % branch)
+            slots = slice(e * C + s * HALF, e * C + (s + 1) * HALF)
             for t in range(PACK):
                 for g in range(KP):
-                    w_codes, w_scales = w_mx[which, e, g, q]
-                    x_codes, x_scales = x_mx[e, g]
+                    w_codes, w_scales = w_mx[branch, e, g, q]
+                    x_codes, x_scales = x_mx[g]
                     nc.tensor.matmul_mx(
                         out=bank[:, t, :],
                         lhsT=w_codes[:, t * P : (t + 1) * P].bitcast(FP8X4),
                         lhsT_scale=w_scales[:, t * P : (t + 1) * P],
-                        rhs=x_codes[:, cols].bitcast(FP8X4),
-                        rhs_scale=x_scales[:, cols],
+                        rhs=x_codes[:, slots].bitcast(FP8X4),
+                        rhs_scale=x_scales[:, slots],
                         start=(g == 0),
                         stop=(g == KP - 1),
                     )
             return bank[:].rearrange("p t n -> p n t")
 
         def linear_branch(e, q, s, spent):
-            sums = first_layer(3, e, q, s)
+            sums = first_layer(LINEAR, e, q, s)
             held = spent[:, s, :].rearrange("p (n t) -> p n t", t=PACK)
             nc.scalar.copy(out=held, in_=sums)
             b_sb[e, q, s] = held
 
         def hidden(e, q, s, spent=None):
-            sums = first_layer(1, e, q, s)
+            sums = first_layer(RELU, e, q, s)
             if spent is None:
                 fresh = stage.tile([P, HALF * PACK], BF16, name="h_grouped", align_bytes=64)
                 grouped = fresh[:]
@@ -169,7 +185,7 @@ def tile_moe_pre_glu_relu_kernel(tc, xT, w1, w3, w2, gate, offs, out):
         def quantize_hidden(e, q, s):
             h_mx[e, q, s] = quantize(h_grouped[e, q, s], "h_%d_%d_%d" % (e, q, s))
 
-        def second_layer(e, s, y):
+        def second_layer(e, s, y, copy):
             w_codes, w_scales = w2_mx[e]
             bank = psum_y.tile([P, HALF], F32, name="bank_y")
             for q in range(HP):
@@ -183,78 +199,75 @@ def tile_moe_pre_glu_relu_kernel(tc, xT, w1, w3, w2, gate, offs, out):
                     start=(q == 0),
                     stop=(q == HP - 1),
                 )
-            nc.scalar.copy(out=y[:, s * HALF : (s + 1) * HALF], in_=bank[:])
+            copy(out=y[:, s * HALF : (s + 1) * HALF], in_=bank[:])
 
         def put_back(e, y, first, count):
-            column = (e * C + first) // LIST_COLS
-            entries = offsets[:, column : column + count // LIST_COLS]
-            nc.vector.tensor_copy(out_sb[:].indirect(entries), y[:, first : first + count])
-
-        def finish(e, y, count):
-            for s in range(HALVES):
-                second_layer(e, s, y)
-            for first in range(0, C, count):
-                put_back(e, y, first, count)
+            nc.vector.tensor_copy(out_sb[:].indirect(entries(e * C + first, count)), y[:, first : first + count])
 
         load_x(0)
         nc.sync.dma_start(offsets[:], offs)
-        gate_row = keep.tile([P, PACK], F32, name="gate_row")
-        nc.sync.dma_start(out=gate_row[:], in_=gate[0].rearrange("(p t) -> p t", t=PACK))
-        identity = keep.tile([P, P], F32, name="identity")
-        make_identity(nc, identity[:])
-        spread = psum.tile([P, PACK, P], F32, name="bank_1", bufs=3)
-        for t in range(PACK):
-            nc.tensor.transpose(spread[:, t, :], gate_row[:, t : t + 1].to_broadcast([P, P]), identity[:])
-        nc.scalar.copy(out=gate_sb[:].rearrange("p (n t) -> p n t", t=PACK), in_=spread[:].rearrange("p t n -> p n t"))
-        load_w(3, 0, 0)
+        spread_gate()
+        load_w(LINEAR, 0, 0)
         load_x(1)
         for g in range(KP):
-            for e in range(E):
-                prepare_x(e, g)
-        for e in range(E):
-            last_expert = e == E - 1
-            if e > 0:
-                load_w(3, e, 0)
-            load_w(3, e, 1)
-            load_w(1, e, 0)
-            if last_expert:
-                load_w(1, e, 1, 0, 1)
-                load_w(1, e, 1, 1, 2)
-            else:
-                load_w(1, e, 1)
-            load_w2(e)
+            prepare_x(g)
 
-            prepare_w(3, e, 0, 0, SHARE_ALL if e == 0 else SHARE_MOST)
-            if e > 0:
-                finish(e - 1, w_raw[3, e, 0, 0][:, 0, :C], C)
-            prepare_w(3, e, 0, 1, SHARE_ALL if e == 0 else SHARE_MOST)
+        load_w(LINEAR, 0, 1)
+        for g in range(KP):
+            load_w(RELU, 0, g)
+        load_w2(0)
+        for g in range(KP):
             for q in range(HP):
-                prepare_w(3, e, 1, q, SHARE_CATCH if e == 0 else SHARE_W5)
+                prepare_w(LINEAR, 0, g, q, SHARE_GATHERING)
+        for g in range(KP):
             for q in range(HP):
-                prepare_w(1, e, 0, q, SHARE_EVEN if last_expert else SHARE_W2)
-            for q in range(1 if last_expert else HP):
-                for s in range(HALVES):
-                    linear_branch(e, q, s, w_raw[1, e, 0, q])
-            prepare_w(1, e, 1, 0, SHARE_EVEN)
-            if last_expert:
-                cast_w(1, e, 1, 1, SHARE_LAST)
-                hidden(e, 0, 0, w_raw[1, e, 1, 1][:, PACK - 1, PASS // 2 :].bitcast(BF16))
-                quantize_w(1, e, 1, 1, PACK)
-                linear_branch(e, 1, 0, w_raw[1, e, 1, 1])
-                prepare_w2(e)
-                linear_branch(e, 1, 1, w_raw[1, e, 1, 1])
-                hidden(e, 0, 1, w_grouped[1, e, 1, 1][:, (PACK - 1) * PASS :])
-            else:
-                prepare_w(1, e, 1, 1, SHARE_EVEN)
-                prepare_w2(e)
-                for s in range(HALVES):
-                    hidden(e, 0, s)
-            hidden(e, 1, 0)
+                prepare_w(RELU, 0, g, q, SHARE_CATCHING_UP if g == 0 else SHARE_EVEN)
+            for s in range(HALVES):
+                linear_branch(0, g, s, w_raw[RELU, 0, g, 0])
+        prepare_w2(0)
+        for s in range(HALVES):
+            hidden(0, 0, s)
+        for s in range(HALVES):
+            hidden(0, 1, s)
             for q in range(HP):
-                quantize_hidden(e, q, 0)
-            hidden(e, 1, 1)
-            for q in range(HP):
-                quantize_hidden(e, q, 1)
-        last_y = keep.tile([P, C], F32, name="last_y")
-        finish(E - 1, last_y[:], HALF)
+                quantize_hidden(0, q, s)
+
+        for g in range(KP):
+            load_w(LINEAR, 1, g)
+        load_w(RELU, 1, 0)
+        for q in range(HP):
+            load_w(RELU, 1, 1, q, q + 1)
+        load_w2(1)
+        prepare_w(LINEAR, 1, 0, 0, SHARE_HIDDEN)
+        first_y = w_raw[LINEAR, 1, 0, 0][:, 0, :C]
+        for s in range(HALVES):
+            second_layer(0, s, first_y, nc.scalar.copy)
+        put_back(0, first_y, 0, C)
+        prepare_w(LINEAR, 1, 0, 1, SHARE_HIDDEN)
+        for q in range(HP):
+            prepare_w(LINEAR, 1, 1, q, SHARE_SCATTERING)
+        for q in range(HP):
+            prepare_w(RELU, 1, 0, q, SHARE_EVEN)
+        for s in range(HALVES):
+            linear_branch(1, 0, s, w_raw[RELU, 1, 0, 0])
+        prepare_w(RELU, 1, 1, 0, SHARE_EVEN)
+
+        last_raw = w_raw[RELU, 1, 1, 1]
+        cast_w(RELU, 1, 1, 1, SHARE_LAST)
+        hidden(1, 0, 0, last_raw[:, PACK - 1, PASS // 2 :].bitcast(BF16))
+        quantize_w(RELU, 1, 1, 1, calls=PACK)
+        linear_branch(1, 1, 0, last_raw)
+        prepare_w2(1)
+        linear_branch(1, 1, 1, last_raw)
+        hidden(1, 0, 1, w_grouped[RELU, 1, 1, 1][:, (PACK - 1) * PASS :])
+        hidden(1, 1, 0)
+        for q in range(HP):
+            quantize_hidden(1, q, 0)
+        hidden(1, 1, 1)
+        second_layer(1, 0, last_y[:], nc.vector.tensor_copy)
+        for q in range(HP):
+            quantize_hidden(1, q, 1)
+        second_layer(1, 1, last_y[:], nc.scalar.copy)
+        for s in range(HALVES):
+            put_back(1, last_y[:], s * HALF, HALF)
         nc.sync.dma_start(out=out, in_=out_sb[:])

@@ -31,7 +31,9 @@ SHARE_CATCHING_UP = 112
 SHARE_HIDDEN = 96
 SHARE_SCATTERING = 80
 SHARE_EVEN = 44
-SHARE_LAST = 56
+H1 = 2
+QC = 4
+SHARE_LAST = 50
 
 RAW_BUFS = 6
 CAST_BUFS = 6
@@ -117,12 +119,15 @@ def tile_moe_pre_glu_relu_kernel(tc, xT, w1, w3, w2, gate, offs, out):
             for q in range(first, last):
                 w_raw[branch, e, g, q] = raw[:, :, (q - first) * PASS : (q - first + 1) * PASS]
 
-        def cast_w(branch, e, g, q, share):
+        def cast_w(branch, e, g, q, share, cut=None):
             grouped = stage.tile([P, PASS * PACK], BF16, name="grouped", align_bytes=64, bufs=CAST_BUFS)
             dst = grouped[:].rearrange("p (t m j) -> p m j t", t=PACK, j=PACK)
             src = w_raw[branch, e, g, q].rearrange("p j (m t) -> p m j t", t=PACK)
             nc.scalar.copy(out=dst[:, :share], in_=src[:, :share])
-            if share < P:
+            if cut is not None:
+                nc.vector.tensor_copy(out=dst[:, cut:], in_=src[:, cut:])
+                nc.vector.tensor_copy(out=dst[:, share:cut], in_=src[:, share:cut])
+            elif share < P:
                 nc.vector.tensor_copy(out=dst[:, share:], in_=src[:, share:])
             w_grouped[branch, e, g, q] = grouped
 
@@ -250,16 +255,17 @@ def tile_moe_pre_glu_relu_kernel(tc, xT, w1, w3, w2, gate, offs, out):
             prepare_w(RELU, 1, 0, q, SHARE_EVEN)
         for s in range(HALVES):
             linear_branch(1, 0, s, w_raw[RELU, 1, 0, 0])
-        prepare_w(RELU, 1, 1, 0, SHARE_EVEN)
+        cast_w(RELU, 1, 1, 0, SHARE_EVEN)
+        quantize_w(RELU, 1, 1, 0, calls=QC)
+        linear_branch(1, 1, 0, w_raw[RELU, 1, 1, 0])
 
         last_raw = w_raw[RELU, 1, 1, 1]
-        cast_w(RELU, 1, 1, 1, SHARE_LAST)
+        cast_w(RELU, 1, 1, 1, SHARE_LAST, P // 2)
         hidden(1, 0, 0, last_raw[:, PACK - 1, PASS // 2 :].bitcast(BF16))
         quantize_w(RELU, 1, 1, 1, calls=PACK)
-        linear_branch(1, 1, 0, last_raw)
         prepare_w2(1)
-        linear_branch(1, 1, 1, last_raw)
-        hidden(1, 0, 1, w_grouped[RELU, 1, 1, 1][:, (PACK - 1) * PASS :])
+        linear_branch(1, 1, 1, w2_raw[1])
+        hidden(1, 0, 1, w_grouped[RELU, 1, 1, 1][:, H1 * PASS : (H1 + 1) * PASS])
         hidden(1, 1, 0)
         for q in range(HP):
             quantize_hidden(1, q, 0)

@@ -33,7 +33,7 @@ SHARE_SCATTERING = 80
 SHARE_EVEN = 44
 H1 = 2
 QC = 4
-SHARE_LAST = 50
+SHARE_LAST = 52
 
 RAW_BUFS = 6
 CAST_BUFS = 6
@@ -121,13 +121,16 @@ def tile_moe_pre_glu_relu_kernel(tc, xT, w1, w3, w2, gate, offs, out):
 
         def cast_w(branch, e, g, q, share, cut=None):
             grouped = stage.tile([P, PASS * PACK], BF16, name="grouped", align_bytes=64, bufs=CAST_BUFS)
-            dst = grouped[:].rearrange("p (t m j) -> p m j t", t=PACK, j=PACK)
-            src = w_raw[branch, e, g, q].rearrange("p j (m t) -> p m j t", t=PACK)
+            dst = grouped[:].rearrange("p (t c i j) -> p c j i t", t=PACK, i=2, j=PACK)
+            src = w_raw[branch, e, g, q].rearrange("p j (c i t) -> p c j i t", i=2, t=PACK)
+            share = share // 2
+            if cut is not None:
+                cut = cut // 2
             nc.scalar.copy(out=dst[:, :share], in_=src[:, :share])
             if cut is not None:
                 nc.vector.tensor_copy(out=dst[:, cut:], in_=src[:, cut:])
                 nc.vector.tensor_copy(out=dst[:, share:cut], in_=src[:, share:cut])
-            elif share < P:
+            elif share < P // 2:
                 nc.vector.tensor_copy(out=dst[:, share:], in_=src[:, share:])
             w_grouped[branch, e, g, q] = grouped
 

@@ -35,6 +35,7 @@ H1 = 2
 QC = 4
 SHARE_LAST = 52
 
+DMA_ALIGN = 256
 RAW_BUFS = 6
 CAST_BUFS = 6
 BRANCH_BANKS = 3
@@ -51,7 +52,7 @@ def tile_moe_pre_glu_relu_kernel(tc, xT, w1, w3, w2, gate, offs, out):
 
         offsets = keep.tile([P, E * C // PER_COLUMN], U16, name="offsets")
         gate_sb = keep.tile([P, E * C], F32, name="gate_sb")
-        out_sb = keep.tile([P, T], F32, name="out_sb")
+        out_sb = keep.tile([P, T], F32, name="out_sb", align_bytes=DMA_ALIGN)
         last_y = keep.tile([P, C], F32, name="last_y")
         x_rows = {}
         x_mx = {}
@@ -91,7 +92,7 @@ def tile_moe_pre_glu_relu_kernel(tc, xT, w1, w3, w2, gate, offs, out):
             nc.scalar.copy(out=gate_sb[:].rearrange("p (n t) -> p n t", t=PACK), in_=spread[:].rearrange("p t n -> p n t"))
 
         def load_x(g):
-            rows = keep.tile([P, PACK * T], F32, name="x_rows_%d" % g)
+            rows = keep.tile([P, PACK * T], F32, name="x_rows_%d" % g, align_bytes=DMA_ALIGN)
             nc.sync.dma_start(out=rows[:], in_=xT[g * PASS : (g + 1) * PASS, :].rearrange("(p j) n -> p (j n)", j=PACK))
             x_rows[g] = rows
 
@@ -112,7 +113,7 @@ def tile_moe_pre_glu_relu_kernel(tc, xT, w1, w3, w2, gate, offs, out):
             x_mx[g] = quantize(grouped[:], "x_%d" % g)
 
         def load_w(branch, e, g, first=0, last=HP):
-            raw = stream.tile([P, PACK, (last - first) * PASS], F32, name="raw", align_bytes=64)
+            raw = stream.tile([P, PACK, (last - first) * PASS], F32, name="raw", align_bytes=DMA_ALIGN)
             w = w1 if branch == RELU else w3
             rows = w[e, g * PASS : (g + 1) * PASS, :].rearrange("(p j) c -> p j c", j=PACK)
             nc.sync.dma_start(out=raw[:], in_=rows[:, :, first * PASS : last * PASS])
@@ -142,7 +143,7 @@ def tile_moe_pre_glu_relu_kernel(tc, xT, w1, w3, w2, gate, offs, out):
             quantize_w(branch, e, g, q)
 
         def load_w2(e):
-            raw = stream.tile([P, HP, PACK * N], F32, name="raw", align_bytes=64)
+            raw = stream.tile([P, HP, PACK * N], F32, name="raw", align_bytes=DMA_ALIGN)
             nc.sync.dma_start(out=raw[:], in_=w2[e].rearrange("(q p j) n -> p q (j n)", p=P, j=PACK))
             w2_raw[e] = raw
 

@@ -15,6 +15,7 @@ U8 = mybir.dt.uint8
 FP8X4 = mybir.dt.float8_e4m3fn_x4
 MULT = mybir.AluOpType.mult
 MAX = mybir.AluOpType.max
+COPY = mybir.ActivationFunctionType.Copy
 
 P = 128
 PACK = 4
@@ -33,7 +34,8 @@ SHARE_SCATTERING = 80
 SHARE_EVEN = 44
 H1 = 2
 QC = 4
-SHARE_LAST = 52
+SHORT = 8
+SHARE_LAST = 56
 
 DMA_ALIGN = 256
 RAW_BUFS = 6
@@ -81,6 +83,9 @@ def tile_moe_pre_glu_relu_kernel(tc, xT, w1, w3, w2, gate, offs, out):
         def entries(first, count):
             return offsets[:, first // PER_COLUMN : (first + count) // PER_COLUMN]
 
+        def scalar_copy(out, in_):
+            nc.scalar.activation(out, in_, COPY)
+
         def spread_gate():
             gate_row = keep.tile([P, PACK], F32, name="gate_row")
             nc.sync.dma_start(out=gate_row[:], in_=gate[0].rearrange("(p t) -> p t", t=PACK))
@@ -89,7 +94,7 @@ def tile_moe_pre_glu_relu_kernel(tc, xT, w1, w3, w2, gate, offs, out):
             spread = psum.tile([P, PACK, P], F32, name="bank_%d" % RELU)
             for t in range(PACK):
                 nc.tensor.transpose(spread[:, t, :], gate_row[:, t : t + 1].to_broadcast([P, P]), identity[:])
-            nc.scalar.copy(out=gate_sb[:].rearrange("p (n t) -> p n t", t=PACK), in_=spread[:].rearrange("p t n -> p n t"))
+            scalar_copy(gate_sb[:].rearrange("p (n t) -> p n t", t=PACK), spread[:].rearrange("p t n -> p n t"))
 
         def load_x(g):
             rows = keep.tile([P, PACK * T], F32, name="x_rows_%d" % g, align_bytes=DMA_ALIGN)
@@ -158,8 +163,10 @@ def tile_moe_pre_glu_relu_kernel(tc, xT, w1, w3, w2, gate, offs, out):
         def first_layer(branch, e, q, s):
             bank = psum.tile([P, PACK, HALF], F32, name="bank_%d" % branch)
             slots = slice(e * C + s * HALF, e * C + (s + 1) * HALF)
-            for t in range(PACK):
-                for g in range(KP):
+            early = (branch, e, q) == (RELU, 1, 0)
+            for outer in range(KP if early else PACK):
+                for inner in range(PACK if early else KP):
+                    g, t = (outer, inner) if early else (inner, outer)
                     w_codes, w_scales = w_mx[branch, e, g, q]
                     x_codes, x_scales = x_mx[g]
                     nc.tensor.matmul_mx(
@@ -168,8 +175,8 @@ def tile_moe_pre_glu_relu_kernel(tc, xT, w1, w3, w2, gate, offs, out):
                         lhsT_scale=w_scales[:, t * P : (t + 1) * P],
                         rhs=x_codes[:, slots].bitcast(FP8X4),
                         rhs_scale=x_scales[:, slots],
-                        start=(g == 0),
-                        stop=(g == KP - 1),
+                        start=(g == 0 and (t == 0 or not early)),
+                        stop=(g == KP - 1 and (t == PACK - 1 or not early)),
                     )
             return bank[:].rearrange("p t n -> p n t")
 
@@ -210,8 +217,8 @@ def tile_moe_pre_glu_relu_kernel(tc, xT, w1, w3, w2, gate, offs, out):
                 )
             copy(out=y[:, s * HALF : (s + 1) * HALF], in_=bank[:])
 
-        def put_back(e, y, first, count):
-            nc.vector.tensor_copy(out_sb[:].indirect(entries(e * C + first, count)), y[:, first : first + count])
+        def put_back(e, y, first, count, copy=nc.vector.tensor_copy):
+            copy(out_sb[:].indirect(entries(e * C + first, count)), y[:, first : first + count])
 
         load_x(0)
         nc.sync.dma_start(offsets[:], offs)
@@ -244,8 +251,10 @@ def tile_moe_pre_glu_relu_kernel(tc, xT, w1, w3, w2, gate, offs, out):
         for g in range(KP):
             load_w(LINEAR, 1, g)
         load_w(RELU, 1, 0)
-        for q in range(HP):
-            load_w(RELU, 1, 1, q, q + 1)
+        load_w(RELU, 1, 1, 0, 1)
+        last_raw = stream.tile([P, PACK * PASS + PASS // 2 - SHORT * 8], F32, name="raw", align_bytes=DMA_ALIGN)
+        w_raw[RELU, 1, 1, 1] = last_raw[:, : PACK * PASS].rearrange("p (j c) -> p j c", j=PACK)
+        nc.sync.dma_start(out=w_raw[RELU, 1, 1, 1], in_=w1[1, PASS:, :].rearrange("(p j) c -> p j c", j=PACK)[:, :, PASS:])
         load_w2(1)
         prepare_w(LINEAR, 1, 0, 0, SHARE_HIDDEN)
         first_y = w_raw[LINEAR, 1, 0, 0][:, 0, :C]
@@ -263,9 +272,8 @@ def tile_moe_pre_glu_relu_kernel(tc, xT, w1, w3, w2, gate, offs, out):
         quantize_w(RELU, 1, 1, 0, calls=QC)
         linear_branch(1, 1, 0, w_raw[RELU, 1, 1, 0])
 
-        last_raw = w_raw[RELU, 1, 1, 1]
-        cast_w(RELU, 1, 1, 1, SHARE_LAST, P // 2)
-        hidden(1, 0, 0, last_raw[:, PACK - 1, PASS // 2 :].bitcast(BF16))
+        cast_w(RELU, 1, 1, 1, SHARE_LAST, P - 2 * SHORT)
+        hidden(1, 0, 0, last_raw[:, PACK * PASS - SHORT * 8 :].bitcast(BF16))
         quantize_w(RELU, 1, 1, 1, calls=PACK)
         prepare_w2(1)
         linear_branch(1, 1, 1, w2_raw[1])
@@ -274,10 +282,10 @@ def tile_moe_pre_glu_relu_kernel(tc, xT, w1, w3, w2, gate, offs, out):
         for q in range(HP):
             quantize_hidden(1, q, 0)
         hidden(1, 1, 1)
-        second_layer(1, 0, last_y[:], nc.vector.tensor_copy)
+        second_layer(1, 0, last_y[:], nc.scalar.copy)
+        put_back(1, last_y[:], 0, HALF, scalar_copy)
         for q in range(HP):
             quantize_hidden(1, q, 1)
-        second_layer(1, 1, last_y[:], nc.scalar.copy)
-        for s in range(HALVES):
-            put_back(1, last_y[:], s * HALF, HALF)
+        second_layer(1, 1, last_y[:], nc.vector.tensor_copy)
+        put_back(1, last_y[:], HALF, HALF, scalar_copy)
         nc.sync.dma_start(out=out, in_=out_sb[:])

@@ -32,14 +32,14 @@ SHARE_CATCHING_UP = 112
 SHARE_HIDDEN = 96
 SHARE_SCATTERING = 80
 SHARE_EVEN = 44
-H1 = 2
-QC = 4
+H1 = 1
+QC = 2
 SHORT = 8
 SHARE_LAST = 56
 
 DMA_ALIGN = 256
 RAW_BUFS = 6
-CAST_BUFS = 6
+CAST_BUFS = 4
 BRANCH_BANKS = 3
 
 
@@ -103,10 +103,11 @@ def tile_moe_pre_glu_relu_kernel(tc, xT, w1, w3, w2, gate, offs, out):
 
         def prepare_x(g):
             picked = stage.tile([P, PACK, E * C], F32, name="picked", bufs=1)
-            for j in range(PACK):
-                window = x_rows[g][:, j * T : (j + 1) * T]
-                for e in range(E):
-                    nc.vector.tensor_copy(picked[:, j, e * C : (e + 1) * C], window.indirect(entries(e * C, C)))
+            for j in range(PACK - 1):
+                nc.vector.tensor_copy(picked[:, j, :], x_rows[g][:, j * T : (j + 2) * T].indirect(offsets[:]))
+            for e in range(E):
+                window = x_rows[g][:, (PACK - 1) * T :]
+                nc.vector.tensor_copy(picked[:, PACK - 1, e * C : (e + 1) * C], window.indirect(entries(e * C, C)))
             grouped = stage.tile([P, E * C * PACK], BF16, name="grouped", align_bytes=64, bufs=CAST_BUFS)
             gate_pairs = gate_sb[:].rearrange("p (c i) -> p c i", i=2)
             nc.vector.tensor_tensor(
@@ -125,9 +126,19 @@ def tile_moe_pre_glu_relu_kernel(tc, xT, w1, w3, w2, gate, offs, out):
             for q in range(first, last):
                 w_raw[branch, e, g, q] = raw[:, :, (q - first) * PASS : (q - first + 1) * PASS]
 
-        def cast_w(branch, e, g, q, share, cut=None):
-            grouped = stage.tile([P, PASS * PACK], BF16, name="grouped", align_bytes=64, bufs=CAST_BUFS)
-            dst = grouped[:].rearrange("p (t c i j) -> p c j i t", t=PACK, i=2, j=PACK)
+        def prepare_wide(branch, e, g, shares):
+            both = stage.tile([P, H * PACK], BF16, name="grouped_wide", align_bytes=64, bufs=2)
+            for q, share in enumerate(shares):
+                cast_w(branch, e, g, q, share, None, both[:, q * PASS * PACK : (q + 1) * PASS * PACK])
+            codes, scales = quantize(both[:], "w%d_%d_%d" % (branch, e, g))
+            for q in range(HP):
+                w_mx[branch, e, g, q] = codes[:, q * PASS : (q + 1) * PASS], scales[:, q * PASS : (q + 1) * PASS]
+
+        def cast_w(branch, e, g, q, share, cut=None, grouped=None):
+            if grouped is None:
+                fresh = stage.tile([P, PASS * PACK], BF16, name="grouped", align_bytes=64, bufs=CAST_BUFS)
+                grouped = fresh[:]
+            dst = grouped.rearrange("p (t c i j) -> p c j i t", t=PACK, i=2, j=PACK)
             src = w_raw[branch, e, g, q].rearrange("p j (c i t) -> p c j i t", i=2, t=PACK)
             share = share // 2
             if cut is not None:
@@ -141,7 +152,7 @@ def tile_moe_pre_glu_relu_kernel(tc, xT, w1, w3, w2, gate, offs, out):
             w_grouped[branch, e, g, q] = grouped
 
         def quantize_w(branch, e, g, q, calls=1):
-            w_mx[branch, e, g, q] = quantize(w_grouped[branch, e, g, q][:], "w%d_%d_%d_%d" % (branch, e, g, q), calls)
+            w_mx[branch, e, g, q] = quantize(w_grouped[branch, e, g, q], "w%d_%d_%d_%d" % (branch, e, g, q), calls)
 
         def prepare_w(branch, e, g, q, share):
             cast_w(branch, e, g, q, share)
@@ -163,7 +174,7 @@ def tile_moe_pre_glu_relu_kernel(tc, xT, w1, w3, w2, gate, offs, out):
         def first_layer(branch, e, q, s):
             bank = psum.tile([P, PACK, HALF], F32, name="bank_%d" % branch)
             slots = slice(e * C + s * HALF, e * C + (s + 1) * HALF)
-            early = (branch, e, q) == (RELU, 1, 0)
+            early = (branch, e) == (RELU, 1) and (q, s) != (1, 1)
             for outer in range(KP if early else PACK):
                 for inner in range(PACK if early else KP):
                     g, t = (outer, inner) if early else (inner, outer)
@@ -199,7 +210,8 @@ def tile_moe_pre_glu_relu_kernel(tc, xT, w1, w3, w2, gate, offs, out):
             h_grouped[e, q, s] = grouped
 
         def quantize_hidden(e, q, s):
-            h_mx[e, q, s] = quantize(h_grouped[e, q, s], "h_%d_%d_%d" % (e, q, s))
+            codes, scales = quantize(h_grouped[e, q, s], "h_%d_%d_%d" % (e, q, s))
+            h_mx[e, q, s] = codes[:], scales[:]
 
         def second_layer(e, s, y, copy):
             w_codes, w_scales = w2_mx[e]
@@ -210,8 +222,8 @@ def tile_moe_pre_glu_relu_kernel(tc, xT, w1, w3, w2, gate, offs, out):
                     out=bank[:],
                     lhsT=w_codes[:, q * N : (q + 1) * N].bitcast(FP8X4),
                     lhsT_scale=w_scales[:, q * N : (q + 1) * N],
-                    rhs=h_codes[:].bitcast(FP8X4),
-                    rhs_scale=h_scales[:],
+                    rhs=h_codes.bitcast(FP8X4),
+                    rhs_scale=h_scales,
                     start=(q == 0),
                     stop=(q == HP - 1),
                 )
@@ -233,20 +245,23 @@ def tile_moe_pre_glu_relu_kernel(tc, xT, w1, w3, w2, gate, offs, out):
             load_w(RELU, 0, g)
         load_w2(0)
         for g in range(KP):
-            for q in range(HP):
-                prepare_w(LINEAR, 0, g, q, SHARE_GATHERING)
+            prepare_wide(LINEAR, 0, g, (P, P))
         for g in range(KP):
-            for q in range(HP):
-                prepare_w(RELU, 0, g, q, SHARE_CATCHING_UP if g == 0 else SHARE_EVEN)
+            if g == 0:
+                prepare_wide(RELU, 0, g, (P, 96))
+            else:
+                for q in range(HP):
+                    prepare_w(RELU, 0, g, q, SHARE_EVEN)
             for s in range(HALVES):
                 linear_branch(0, g, s, w_raw[RELU, 0, g, 0])
         prepare_w2(0)
-        for s in range(HALVES):
-            hidden(0, 0, s)
-        for s in range(HALVES):
-            hidden(0, 1, s)
-            for q in range(HP):
-                quantize_hidden(0, q, s)
+        for q in range(HP):
+            both = stage.tile([P, C * PACK], BF16, name="h_both", align_bytes=64, bufs=HP)
+            for s in range(HALVES):
+                hidden(0, q, s, both[:, s * PASS : (s + 1) * PASS])
+            codes, scales = quantize(both[:], "h_0_%d" % q)
+            for s in range(HALVES):
+                h_mx[0, q, s] = codes[:, s * HALF : (s + 1) * HALF], scales[:, s * HALF : (s + 1) * HALF]
 
         for g in range(KP):
             load_w(LINEAR, 1, g)
@@ -256,12 +271,12 @@ def tile_moe_pre_glu_relu_kernel(tc, xT, w1, w3, w2, gate, offs, out):
         w_raw[RELU, 1, 1, 1] = last_raw[:, : PACK * PASS].rearrange("p (j c) -> p j c", j=PACK)
         nc.sync.dma_start(out=w_raw[RELU, 1, 1, 1], in_=w1[1, PASS:, :].rearrange("(p j) c -> p j c", j=PACK)[:, :, PASS:])
         load_w2(1)
-        prepare_w(LINEAR, 1, 0, 0, SHARE_HIDDEN)
+        prepare_w(LINEAR, 1, 0, 0, P)
         first_y = w_raw[LINEAR, 1, 0, 0][:, 0, :C]
         for s in range(HALVES):
             second_layer(0, s, first_y, nc.scalar.copy)
         put_back(0, first_y, 0, C)
-        prepare_w(LINEAR, 1, 0, 1, SHARE_HIDDEN)
+        prepare_w(LINEAR, 1, 0, 1, 64)
         for q in range(HP):
             prepare_w(LINEAR, 1, 1, q, SHARE_SCATTERING)
         for q in range(HP):
@@ -274,7 +289,7 @@ def tile_moe_pre_glu_relu_kernel(tc, xT, w1, w3, w2, gate, offs, out):
 
         cast_w(RELU, 1, 1, 1, SHARE_LAST, P - 2 * SHORT)
         hidden(1, 0, 0, last_raw[:, PACK * PASS - SHORT * 8 :].bitcast(BF16))
-        quantize_w(RELU, 1, 1, 1, calls=PACK)
+        quantize_w(RELU, 1, 1, 1, calls=2)
         prepare_w2(1)
         linear_branch(1, 1, 1, w2_raw[1])
         hidden(1, 0, 1, w_grouped[RELU, 1, 1, 1][:, H1 * PASS : (H1 + 1) * PASS])

@@ -143,7 +143,8 @@ def tile_moe_pre_glu_relu_kernel(tc, xT, w1, w3, w2, gate, offs, out):
             share = share // 2
             if cut is not None:
                 cut = cut // 2
-            nc.scalar.copy(out=dst[:, :share], in_=src[:, :share])
+            if share > 0:
+                nc.scalar.copy(out=dst[:, :share], in_=src[:, :share])
             if cut is not None:
                 nc.vector.tensor_copy(out=dst[:, cut:], in_=src[:, cut:])
                 nc.vector.tensor_copy(out=dst[:, share:cut], in_=src[:, share:cut])
@@ -272,13 +273,13 @@ def tile_moe_pre_glu_relu_kernel(tc, xT, w1, w3, w2, gate, offs, out):
         nc.sync.dma_start(out=w_raw[RELU, 1, 1, 1], in_=w1[1, PASS:, :].rearrange("(p j) c -> p j c", j=PACK)[:, :, PASS:])
         load_w2(1)
         prepare_w(LINEAR, 1, 0, 0, P)
-        first_y = w_raw[LINEAR, 1, 0, 0][:, 0, :C]
+        prepare_w(LINEAR, 1, 0, 1, 64)
+        first_y = w_raw[LINEAR, 1, 0, 1][:, 0, :C]
         for s in range(HALVES):
             second_layer(0, s, first_y, nc.scalar.copy)
-        put_back(0, first_y, 0, C)
-        prepare_w(LINEAR, 1, 0, 1, 64)
-        for q in range(HP):
-            prepare_w(LINEAR, 1, 1, q, SHARE_SCATTERING)
+        put_back(0, first_y, 0, C, scalar_copy)
+        for q, share in enumerate((0, 44)):
+            prepare_w(LINEAR, 1, 1, q, share)
         for q in range(HP):
             prepare_w(RELU, 1, 0, q, SHARE_EVEN)
         for s in range(HALVES):

@@ -91,7 +91,7 @@ def tile_moe_pre_glu_relu_kernel(tc, xT, w1, w3, w2, gate, offs, out):
             nc.sync.dma_start(out=gate_row[:], in_=gate[0].rearrange("(p t) -> p t", t=PACK))
             identity = keep.tile([P, P], F32, name="identity")
             make_identity(nc, identity[:])
-            spread = psum.tile([P, PACK, P], F32, name="bank_%d" % RELU)
+            spread = psum.tile([P, PACK, P], F32, name="bank_a0", bufs=1)
             for t in range(PACK):
                 nc.tensor.transpose(spread[:, t, :], gate_row[:, t : t + 1].to_broadcast([P, P]), identity[:])
             scalar_copy(gate_sb[:].rearrange("p (n t) -> p n t", t=PACK), spread[:].rearrange("p t n -> p n t"))
@@ -173,7 +173,10 @@ def tile_moe_pre_glu_relu_kernel(tc, xT, w1, w3, w2, gate, offs, out):
             w2_mx[e] = quantize(grouped[:], "w2_%d" % e)
 
         def first_layer(branch, e, q, s):
-            bank = psum.tile([P, PACK, HALF], F32, name="bank_%d" % branch)
+            if branch == LINEAR:
+                bank = psum.tile([P, PACK, HALF], F32, name="bank_b")
+            else:
+                bank = psum.tile([P, PACK, HALF], F32, name="bank_a%d" % ((2 + 4 * e + 2 * q + s - 1) % BRANCH_BANKS), bufs=1)
             slots = slice(e * C + s * HALF, e * C + (s + 1) * HALF)
             early = (branch, e) == (RELU, 1) and (q, s) != (1, 1)
             for outer in range(KP if early else PACK):
@@ -209,6 +212,21 @@ def tile_moe_pre_glu_relu_kernel(tc, xT, w1, w3, w2, gate, offs, out):
                 out=grouped.rearrange("p (n t) -> p n t", t=PACK), in0=sums, scalar=0.0, in1=b_sb[e, q, s], op0=MAX, op1=MULT
             )
             h_grouped[e, q, s] = grouped
+
+        def warm_up():
+            idle = psum.tile([P, E * C], F32, name="bank_a0", bufs=1)
+            w_codes, w_scales = w_mx[RELU, 1, 1, 1]
+            x_codes, x_scales = x_mx[0]
+            for t in range(2):
+                nc.tensor.matmul_mx(
+                    out=idle[:],
+                    lhsT=w_codes[:, t * P : (t + 1) * P].bitcast(FP8X4),
+                    lhsT_scale=w_scales[:, t * P : (t + 1) * P],
+                    rhs=x_codes[:].bitcast(FP8X4),
+                    rhs_scale=x_scales[:],
+                    start=(t == 0),
+                    stop=(t == 1),
+                )
 
         def quantize_hidden(e, q, s):
             codes, scales = quantize(h_grouped[e, q, s], "h_%d_%d_%d" % (e, q, s))
@@ -294,6 +312,7 @@ def tile_moe_pre_glu_relu_kernel(tc, xT, w1, w3, w2, gate, offs, out):
         prepare_w2(1)
         linear_branch(1, 1, 1, w2_raw[1])
         hidden(1, 0, 1, w_grouped[RELU, 1, 1, 1][:, H1 * PASS : (H1 + 1) * PASS])
+        warm_up()
         hidden(1, 1, 0)
         for q in range(HP):
             quantize_hidden(1, q, 0)
@@ -303,5 +322,5 @@ def tile_moe_pre_glu_relu_kernel(tc, xT, w1, w3, w2, gate, offs, out):
         for q in range(HP):
             quantize_hidden(1, q, 1)
         second_layer(1, 1, last_y[:], nc.vector.tensor_copy)
-        put_back(1, last_y[:], HALF, HALF, scalar_copy)
+        put_back(1, last_y[:], HALF, HALF)
         nc.sync.dma_start(out=out, in_=out_sb[:])

@@ -213,21 +213,6 @@ def tile_moe_pre_glu_relu_kernel(tc, xT, w1, w3, w2, gate, offs, out):
             )
             h_grouped[e, q, s] = grouped
 
-        def warm_up():
-            idle = psum.tile([P, E * C], F32, name="bank_a0", bufs=1)
-            w_codes, w_scales = w_mx[RELU, 1, 1, 1]
-            x_codes, x_scales = x_mx[0]
-            for t in range(2):
-                nc.tensor.matmul_mx(
-                    out=idle[:],
-                    lhsT=w_codes[:, t * P : (t + 1) * P].bitcast(FP8X4),
-                    lhsT_scale=w_scales[:, t * P : (t + 1) * P],
-                    rhs=x_codes[:].bitcast(FP8X4),
-                    rhs_scale=x_scales[:],
-                    start=(t == 0),
-                    stop=(t == 1),
-                )
-
         def quantize_hidden(e, q, s):
             codes, scales = quantize(h_grouped[e, q, s], "h_%d_%d_%d" % (e, q, s))
             h_mx[e, q, s] = codes[:], scales[:]
@@ -312,7 +297,6 @@ def tile_moe_pre_glu_relu_kernel(tc, xT, w1, w3, w2, gate, offs, out):
         prepare_w2(1)
         linear_branch(1, 1, 1, w2_raw[1])
         hidden(1, 0, 1, w_grouped[RELU, 1, 1, 1][:, H1 * PASS : (H1 + 1) * PASS])
-        warm_up()
         hidden(1, 1, 0)
         for q in range(HP):
             quantize_hidden(1, q, 0)

from contextlib import ExitStack

import concourse.mybir as mybir
from concourse.masks import make_identity

K, T, E, C, H, N = 1024, 512, 2, 256, 1024, 128
FLOPS = 2 * E * C * (2 * K * H + H * N)
BYTES = 4 * (K * T + 2 * E * K * H + E * H * N + E * C + N * T) + 2 * 128 * 32

F32 = mybir.dt.float32
BF16 = mybir.dt.bfloat16
U32 = mybir.dt.uint32
U16 = mybir.dt.uint16
U8 = mybir.dt.uint8
FP8X4 = mybir.dt.float8_e4m3fn_x4
MULT = mybir.AluOpType.mult
MAX = mybir.AluOpType.max
COPY = mybir.ActivationFunctionType.Copy

P = 128
PACK = 4
PASS = P * PACK
KP = K // PASS
HP = H // PASS
HALF = 128
HALVES = C // HALF
PER_COLUMN = 16
RELU, LINEAR = 1, 3

SHARE_GATHERING = 128
SHARE_CATCHING_UP = 112
SHARE_HIDDEN = 96
SHARE_SCATTERING = 80
SHARE_EVEN = 44
H1 = 1
QC = 2
SHORT = 8
SHARE_LAST = 56

DMA_ALIGN = 256
RAW_BUFS = 6
CAST_BUFS = 4
BRANCH_BANKS = 3


def tile_moe_pre_glu_relu_kernel(tc, xT, w1, w3, w2, gate, offs, out):
    nc = tc.nc
    with ExitStack() as ctx:
        keep = ctx.enter_context(tc.tile_pool(name="keep", bufs=1))
        stream = ctx.enter_context(tc.tile_pool(name="stream", bufs=RAW_BUFS))
        stage = ctx.enter_context(tc.tile_pool(name="stage", bufs=HP * HALVES))
        psum = ctx.enter_context(tc.psum_pool(name="psum", bufs=BRANCH_BANKS))
        psum_y = ctx.enter_context(tc.psum_pool(name="psum_y", bufs=HALVES))

        offsets = keep.tile([P, E * C // PER_COLUMN], U16, name="offsets")
        gate_sb = keep.tile([P, E * C], F32, name="gate_sb")
        out_sb = keep.tile([P, T], F32, name="out_sb", align_bytes=DMA_ALIGN)
        last_y = keep.tile([P, C], F32, name="last_y")
        x_rows = {}
        x_mx = {}
        w_raw = {}
        w_grouped = {}
        w_mx = {}
        w2_raw = {}
        w2_mx = {}
        b_sb = {}
        h_grouped = {}
        h_mx = {}

        def quantize(grouped, name, calls=1):
            words = grouped.shape[1] // PACK
            codes = keep.tile([P, words], U32, name=name + "_codes", align_bytes=64)
            scales = keep.tile([P, words], U8, name=name + "_scales", align_bytes=64)
            step = words // calls
            for c in range(0, words, step):
                nc.vector.quantize_mx(
                    out=codes[:, c : c + step].bitcast(FP8X4),
                    scales=scales[:, c : c + step],
                    in_=grouped[:, c * PACK : (c + step) * PACK],
                )
            return codes, scales

        def entries(first, count):
            return offsets[:, first // PER_COLUMN : (first + count) // PER_COLUMN]

        def scalar_copy(out, in_):
            nc.scalar.activation(out, in_, COPY)

        def spread_gate():
            gate_row = keep.tile([P, PACK], F32, name="gate_row")
            nc.sync.dma_start(out=gate_row[:], in_=gate[0].rearrange("(p t) -> p t", t=PACK))
            identity = keep.tile([P, P], F32, name="identity")
            make_identity(nc, identity[:])
            spread = psum.tile([P, PACK, P], F32, name="bank_a0", bufs=1)
            for t in range(PACK):
                nc.tensor.transpose(spread[:, t, :], gate_row[:, t : t + 1].to_broadcast([P, P]), identity[:])
            scalar_copy(gate_sb[:].rearrange("p (n t) -> p n t", t=PACK), spread[:].rearrange("p t n -> p n t"))

        def load_x(g):
            rows = keep.tile([P, PACK * T], F32, name="x_rows_%d" % g, align_bytes=DMA_ALIGN)
            nc.sync.dma_start(out=rows[:], in_=xT[g * PASS : (g + 1) * PASS, :].rearrange("(p j) n -> p (j n)", j=PACK))
            x_rows[g] = rows

        def prepare_x(g):
            picked = stage.tile([P, PACK, E * C], F32, name="picked", bufs=1)
            for j in range(PACK - 1):
                nc.vector.tensor_copy(picked[:, j, :], x_rows[g][:, j * T : (j + 2) * T].indirect(offsets[:]))
            for e in range(E):
                window = x_rows[g][:, (PACK - 1) * T :]
                nc.vector.tensor_copy(picked[:, PACK - 1, e * C : (e + 1) * C], window.indirect(entries(e * C, C)))
            grouped = stage.tile([P, E * C * PACK], BF16, name="grouped", align_bytes=64, bufs=CAST_BUFS)
            gate_pairs = gate_sb[:].rearrange("p (c i) -> p c i", i=2)
            nc.vector.tensor_tensor(
                grouped[:].rearrange("p (c i j) -> p c j i", i=2, j=PACK),
                picked[:].rearrange("p j (c i) -> p c j i", i=2),
                gate_pairs.unsqueeze(2).to_broadcast([P, E * C // 2, PACK, 2]),
                MULT,
            )
            x_mx[g] = quantize(grouped[:], "x_%d" % g)

        def load_w(branch, e, g, first=0, last=HP):
            raw = stream.tile([P, PACK, (last - first) * PASS], F32, name="raw", align_bytes=DMA_ALIGN)
            w = w1 if branch == RELU else w3
            rows = w[e, g * PASS : (g + 1) * PASS, :].rearrange("(p j) c -> p j c", j=PACK)
            nc.sync.dma_start(out=raw[:], in_=rows[:, :, first * PASS : last * PASS])
            for q in range(first, last):
                w_raw[branch, e, g, q] = raw[:, :, (q - first) * PASS : (q - first + 1) * PASS]

        def prepare_wide(branch, e, g, shares):
            both = stage.tile([P, H * PACK], BF16, name="grouped_wide", align_bytes=64, bufs=2)
            for q, share in enumerate(shares):
                cast_w(branch, e, g, q, share, None, both[:, q * PASS * PACK : (q + 1) * PASS * PACK])
            codes, scales = quantize(both[:], "w%d_%d_%d" % (branch, e, g))
            for q in range(HP):
                w_mx[branch, e, g, q] = codes[:, q * PASS : (q + 1) * PASS], scales[:, q * PASS : (q + 1) * PASS]

        def cast_w(branch, e, g, q, share, cut=None, grouped=None):
            if grouped is None:
                fresh = stage.tile([P, PASS * PACK], BF16, name="grouped", align_bytes=64, bufs=CAST_BUFS)
                grouped = fresh[:]
            dst = grouped.rearrange("p (t c i j) -> p c j i t", t=PACK, i=2, j=PACK)
            src = w_raw[branch, e, g, q].rearrange("p j (c i t) -> p c j i t", i=2, t=PACK)
            share = share // 2
            if cut is not None:
                cut = cut // 2
            if share > 0:
                nc.scalar.copy(out=dst[:, :share], in_=src[:, :share])
            if cut is not None:
                nc.vector.tensor_copy(out=dst[:, cut:], in_=src[:, cut:])
                nc.vector.tensor_copy(out=dst[:, share:cut], in_=src[:, share:cut])
            elif share < P // 2:
                nc.vector.tensor_copy(out=dst[:, share:], in_=src[:, share:])
            w_grouped[branch, e, g, q] = grouped

        def quantize_w(branch, e, g, q, calls=1):
            w_mx[branch, e, g, q] = quantize(w_grouped[branch, e, g, q], "w%d_%d_%d_%d" % (branch, e, g, q), calls)

        def prepare_w(branch, e, g, q, share):
            cast_w(branch, e, g, q, share)
            quantize_w(branch, e, g, q)

        def load_w2(e):
            raw = stream.tile([P, HP, PACK * N], F32, name="raw", align_bytes=DMA_ALIGN)
            nc.sync.dma_start(out=raw[:], in_=w2[e].rearrange("(q p j) n -> p q (j n)", p=P, j=PACK))
            w2_raw[e] = raw

        def prepare_w2(e):
            grouped = stage.tile([P, HP * N * PACK], BF16, name="w2_grouped", align_bytes=64, bufs=E)
            nc.scalar.copy(
                out=grouped[:].rearrange("p (q c i j) -> p q c j i", q=HP, i=4, j=PACK),
                in_=w2_raw[e][:].rearrange("p q (j c i) -> p q c j i", j=PACK, i=4),
            )
            w2_mx[e] = quantize(grouped[:], "w2_%d" % e)

        def first_layer(branch, e, q, s):
            if branch == LINEAR:
                bank = psum.tile([P, PACK, HALF], F32, name="bank_b")
            else:
                bank = psum.tile([P, PACK, HALF], F32, name="bank_a%d" % ((2 + 4 * e + 2 * q + s - 1) % BRANCH_BANKS), bufs=1)
            slots = slice(e * C + s * HALF, e * C + (s + 1) * HALF)
            early = (branch, e) == (RELU, 1) and (q, s) != (1, 1)
            for outer in range(KP if early else PACK):
                for inner in range(PACK if early else KP):
                    g, t = (outer, inner) if early else (inner, outer)
                    w_codes, w_scales = w_mx[branch, e, g, q]
                    x_codes, x_scales = x_mx[g]
                    nc.tensor.matmul_mx(
                        out=bank[:, t, :],
                        lhsT=w_codes[:, t * P : (t + 1) * P].bitcast(FP8X4),
                        lhsT_scale=w_scales[:, t * P : (t + 1) * P],
                        rhs=x_codes[:, slots].bitcast(FP8X4),
                        rhs_scale=x_scales[:, slots],
                        start=(g == 0 and (t == 0 or not early)),
                        stop=(g == KP - 1 and (t == PACK - 1 or not early)),
                    )
            return bank[:].rearrange("p t n -> p n t")

        def linear_branch(e, q, s, spent):
            sums = first_layer(LINEAR, e, q, s)
            held = spent[:, s, :].rearrange("p (n t) -> p n t", t=PACK)
            nc.scalar.copy(out=held, in_=sums)
            b_sb[e, q, s] = held

        def hidden(e, q, s, spent=None):
            sums = first_layer(RELU, e, q, s)
            if spent is None:
                fresh = stage.tile([P, HALF * PACK], BF16, name="h_grouped", align_bytes=64)
                grouped = fresh[:]
            else:
                grouped = spent
            nc.vector.scalar_tensor_tensor(
                out=grouped.rearrange("p (n t) -> p n t", t=PACK), in0=sums, scalar=0.0, in1=b_sb[e, q, s], op0=MAX, op1=MULT
            )
            h_grouped[e, q, s] = grouped

        def quantize_hidden(e, q, s):
            codes, scales = quantize(h_grouped[e, q, s], "h_%d_%d_%d" % (e, q, s))
            h_mx[e, q, s] = codes[:], scales[:]

        def second_layer(e, s, y, copy):
            w_codes, w_scales = w2_mx[e]
            bank = psum_y.tile([P, HALF], F32, name="bank_y")
            for q in range(HP):
                h_codes, h_scales = h_mx[e, q, s]
                nc.tensor.matmul_mx(
                    out=bank[:],
                    lhsT=w_codes[:, q * N : (q + 1) * N].bitcast(FP8X4),
                    lhsT_scale=w_scales[:, q * N : (q + 1) * N],
                    rhs=h_codes.bitcast(FP8X4),
                    rhs_scale=h_scales,
                    start=(q == 0),
                    stop=(q == HP - 1),
                )
            copy(out=y[:, s * HALF : (s + 1) * HALF], in_=bank[:])

        def put_back(e, y, first, count, copy=nc.vector.tensor_copy):
            copy(out_sb[:].indirect(entries(e * C + first, count)), y[:, first : first + count])

        load_x(0)
        nc.sync.dma_start(offsets[:], offs)
        spread_gate()
        load_w(LINEAR, 0, 0)
        load_x(1)
        for g in range(KP):
            prepare_x(g)

        load_w(LINEAR, 0, 1)
        for g in range(KP):
            load_w(RELU, 0, g)
        load_w2(0)
        for g in range(KP):
            prepare_wide(LINEAR, 0, g, (P, P))
        for g in range(KP):
            if g == 0:
                prepare_wide(RELU, 0, g, (P, 96))
            else:
                for q in range(HP):
                    prepare_w(RELU, 0, g, q, SHARE_EVEN)
            for s in range(HALVES):
                linear_branch(0, g, s, w_raw[RELU, 0, g, 0])
        prepare_w2(0)
        for q in range(HP):
            both = stage.tile([P, C * PACK], BF16, name="h_both", align_bytes=64, bufs=HP)
            for s in range(HALVES):
                hidden(0, q, s, both[:, s * PASS : (s + 1) * PASS])
            codes, scales = quantize(both[:], "h_0_%d" % q)
            for s in range(HALVES):
                h_mx[0, q, s] = codes[:, s * HALF : (s + 1) * HALF], scales[:, s * HALF : (s + 1) * HALF]

        for g in range(KP):
            load_w(LINEAR, 1, g)
        load_w(RELU, 1, 0)
        load_w(RELU, 1, 1, 0, 1)
        last_raw = stream.tile([P, PACK * PASS + PASS // 2 - SHORT * 8], F32, name="raw", align_bytes=DMA_ALIGN)
        w_raw[RELU, 1, 1, 1] = last_raw[:, : PACK * PASS].rearrange("p (j c) -> p j c", j=PACK)
        nc.sync.dma_start(out=w_raw[RELU, 1, 1, 1], in_=w1[1, PASS:, :].rearrange("(p j) c -> p j c", j=PACK)[:, :, PASS:])
        load_w2(1)
        prepare_w(LINEAR, 1, 0, 0, P)
        prepare_w(LINEAR, 1, 0, 1, 64)
        first_y = w_raw[LINEAR, 1, 0, 1][:, 0, :C]
        for s in range(HALVES):
            second_layer(0, s, first_y, nc.scalar.copy)
        put_back(0, first_y, 0, C, scalar_copy)
        for q, share in enumerate((0, 44)):
            prepare_w(LINEAR, 1, 1, q, share)
        for q in range(HP):
            prepare_w(RELU, 1, 0, q, SHARE_EVEN)
        for s in range(HALVES):
            linear_branch(1, 0, s, w_raw[RELU, 1, 0, 0])
        cast_w(RELU, 1, 1, 0, SHARE_EVEN)
        quantize_w(RELU, 1, 1, 0, calls=QC)
        linear_branch(1, 1, 0, w_raw[RELU, 1, 1, 0])

        cast_w(RELU, 1, 1, 1, SHARE_LAST, P - 2 * SHORT)
        hidden(1, 0, 0, last_raw[:, PACK * PASS - SHORT * 8 :].bitcast(BF16))
        quantize_w(RELU, 1, 1, 1, calls=2)
        prepare_w2(1)
        linear_branch(1, 1, 1, w2_raw[1])
        hidden(1, 0, 1, w_grouped[RELU, 1, 1, 1][:, H1 * PASS : (H1 + 1) * PASS])
        hidden(1, 1, 0)
        for q in range(HP):
            quantize_hidden(1, q, 0)
        hidden(1, 1, 1)
        second_layer(1, 0, last_y[:], nc.scalar.copy)
        put_back(1, last_y[:], 0, HALF, scalar_copy)
        for q in range(HP):
            quantize_hidden(1, q, 1)
        second_layer(1, 1, last_y[:], nc.vector.tensor_copy)
        put_back(1, last_y[:], HALF, HALF)
        nc.sync.dma_start(out=out, in_=out_sb[:])
